import numpy as np
import ml_dtypes


def mxq(x, axis, fmt="e4m3"):
    dtype, down = {"e4m3": (ml_dtypes.float8_e4m3fn, 7), "e5m2": (ml_dtypes.float8_e5m2, 14)}[fmt]
    v = np.moveaxis(np.asarray(x, np.float32).astype(ml_dtypes.bfloat16).astype(np.float64), axis, -1)
    blocks = v.reshape(v.shape[:-1] + (-1, 32))
    amax = np.abs(blocks).max(-1, keepdims=True)
    byte = np.maximum(np.where(amax > 0, np.frexp(amax)[1] - 1 + 127, 0) - down, 1)
    scale = np.exp2(byte - 127.0)
    codes = (blocks / scale).astype(np.float32).astype(dtype).astype(np.float64)
    return np.moveaxis((codes * scale).reshape(v.shape), -1, axis)


WIDE = False


def mx_kscale(k):
    if not WIDE:
        return np.ones(k)
    levels = np.array([10, -10, 5, -5, 0])
    if k % 512:
        return np.exp2(np.random.permutation(np.resize(levels, k // 32))).repeat(32)
    a = np.empty((k // 512, 16))
    for p in range(k // 512):
        a[p, :8] = np.random.permutation(np.resize(levels, 8))
        for g in range(8):
            far = levels[np.abs(levels - a[p, g]) >= 10]
            a[p, g + 8] = far[np.random.randint(len(far))]
    return np.exp2(a.ravel()).repeat(32)


def f64(x):
    return np.asarray(x).astype(np.float64)


def striped(idx):
    return np.tile(idx.reshape(-1, 16).T, (8, 1)).astype(np.uint16)


def unstriped(offs):
    return offs[:16].T.reshape(-1).astype(np.int64)


E2M1 = np.array([0.0, 0.5, 1.0, 1.5, 2.0, 3.0, 4.0, 6.0, -0.0, -0.5, -1.0, -1.5, -2.0, -3.0, -4.0, -6.0])


def pack_weight(w, fmt):
    k, n = w.shape
    w = f64(np.asarray(w, np.float32).astype(ml_dtypes.bfloat16)).reshape(k // 32, 32, n)
    amax = np.abs(w).max(1)
    if fmt == "e4m3":
        byte = np.frexp(amax)[1] - 1 + 127 - 7
    else:
        mant, ex = np.frexp(amax / 6.0)
        byte = np.where(mant > 0.5, ex, ex - 1) + 127
    byte = np.clip(np.where(amax > 0, byte, 1), 1, 254)
    scaled = (w * np.exp2(127.0 - byte)[:, None, :]).reshape(k, n).astype(np.float32)
    by_word = np.ascontiguousarray(scaled.reshape(k // 512, 128, 4, n).transpose(0, 1, 3, 2))
    if fmt == "e4m3":
        words = by_word.astype(ml_dtypes.float8_e4m3fn).view(np.uint8)
    else:
        c = by_word.astype(ml_dtypes.float4_e2m1fn).view(np.uint8) & 0xF
        words = (c[..., 0::2] | (c[..., 1::2] << 4)).reshape(k // 512, 128, 2 * n)
    return np.ascontiguousarray(words), np.ascontiguousarray(byte.astype(np.uint8).reshape(k // 512, 16, n))


def unpack_weight(words, scales, fmt):
    g, _, n = scales.shape
    words = np.ascontiguousarray(words).reshape(g, 128, n, -1)
    if fmt == "e4m3":
        vals = words.view(ml_dtypes.float8_e4m3fn).astype(np.float64)
    else:
        nib = np.empty((g, 128, n, 4), np.uint8)
        nib[..., 0::2] = words & 0xF
        nib[..., 1::2] = words >> 4
        vals = E2M1[nib]
    vals = vals * np.repeat(np.exp2(scales.astype(np.float64) - 127.0), 8, axis=1)[..., None]
    return vals.transpose(0, 1, 3, 2).reshape(g * 512, n)


def silu(v):
    return v / (1.0 + np.exp(-np.maximum(v, -700.0)))


K, T, E, C, H, N, TOP = 1536, 512, 6, 256, 512, 128, 3


def by_expert(wq, xq):
    return np.concatenate([wq[e].T @ xq[:, e * C:(e + 1) * C] for e in range(E)], axis=1)


def setup_inputs():
    n = np.random.standard_normal
    s = mx_kscale(K)
    u = mx_kscale(H)
    deal = np.repeat(np.arange(E), C).reshape(TOP, T)[:, np.random.permutation(T)]
    deal = np.take_along_axis(deal, np.argsort(np.random.rand(TOP, T), axis=0), axis=0)
    for _ in range(8):
        s_, t_ = np.random.permutation(T).reshape(2, -1); r = np.random.randint(TOP, size=T // 2); x, y = deal[r, s_].copy(), deal[r, t_].copy()
        ok = ~((deal[:, s_] == y).any(0) | (deal[:, t_] == x).any(0)); deal[r[ok], s_[ok]] = y[ok]; deal[r[ok], t_[ok]] = x[ok]
    order = np.argsort(deal.reshape(-1) + 0.5 * np.random.rand(TOP * T))
    slot_token = order % T; pos = np.empty(TOP * T, np.int64); pos[order] = np.arange(TOP * T); pos = pos.reshape(TOP, T)
    g = np.random.uniform(0.5, 1.5, (TOP, T)); g = g / g.sum(0)
    x = pack_weight(n((K, T)) * s[:, None], "e4m3")
    w = [pack_weight(m, "e2m1") for m in n((E, K, N)) / np.sqrt(K) / s[None, :, None]]
    wa = [pack_weight(m, "e4m3") for m in n((E, K, H)) / np.sqrt(K) / s[None, :, None] * u]
    return {
        "x_words": x[0],
        "x_scales": x[1],
        "w_words": np.stack([m[0] for m in w]),
        "w_scales": np.stack([m[1] for m in w]),
        "wa_words": np.stack([m[0] for m in wa]),
        "wa_scales": np.stack([m[1] for m in wa]),
        "wb": (n((E, H, N)) / np.sqrt(H) / u[None, :, None]).astype(np.float32),
        "gate": np.stack([np.tile(r, (128, 1)) for r in g]).astype(np.float32),
        "offs": striped(slot_token),
        "pos1": striped(pos[0]),
        "pos2": striped(pos[1]),
        "pos3": striped(pos[2]),
    }


def reference(x_words, x_scales, w_words, w_scales, wa_words, wa_scales, wb, gate, offs, pos1, pos2, pos3):
    w = np.stack([unpack_weight(w_words[e], w_scales[e], "e2m1") for e in range(E)])
    wa = np.stack([unpack_weight(wa_words[e], wa_scales[e], "e4m3") for e in range(E)])
    wbq = mxq(f64(wb), 1, "e4m3")
    idx = unstriped(offs)
    xq = unpack_weight(x_words, x_scales, "e4m3")[:, idx]
    h = silu(by_expert(wa, xq))
    y = by_expert(w, xq) + by_expert(wbq, mxq(h, 0, "e4m3"))
    out = sum(f64(gate[r, :1]) * y[:, unstriped(p)] for r, p in enumerate((pos1, pos2, pos3)))
    return out

@@ -1,0 +1,269 @@
+from contextlib import ExitStack
+
+import concourse.mybir as mybir
+from concourse.masks import make_identity
+
+K, T, E, C, H, N, TOP = 1536, 512, 6, 256, 512, 128, 3
+P = 128
+PASSES = K // 512
+SLOTS = E * C
+FLOPS = 2 * SLOTS * (K * (H + N) + H * N)
+
+F32 = mybir.dt.float32
+BF16 = mybir.dt.bfloat16
+I32 = mybir.dt.int32
+U32 = mybir.dt.uint32
+U16 = mybir.dt.uint16
+U8 = mybir.dt.uint8
+FP8X4 = mybir.dt.float8_e4m3fn_x4
+FP4X4 = mybir.dt.float4_e2m1fn_x4
+SILU = mybir.ActivationFunctionType.Silu
+MULT = mybir.AluOpType.mult
+ADD = mybir.AluOpType.add
+
+BYTE_GROUPS = ((0, 1), (1, 3), (3, 6))
+LAG = 3
+SHIFT_ROWS = 112
+
+
+def tile_moe_elr_silu_kernel(
+    tc, x_words, x_scales, w_words, w_scales, wa_words, wa_scales, wb, gate, offs, pos1, pos2, pos3, out
+):
+    nc = tc.nc
+    with ExitStack() as ctx:
+        held = ctx.enter_context(tc.tile_pool(name="held", bufs=1))
+        ring = ctx.enter_context(tc.tile_pool(name="ring", bufs=2))
+        psum = ctx.enter_context(tc.psum_pool(name="psum", bufs=1))
+
+        def own(shape, dtype, name, tag=None):
+            return held.tile(shape, dtype, name=name, tag=tag or name, align_bytes=64)
+
+        offs_t = held.tile([P, SLOTS // 16], U16, name="offs_t")
+        nc.sync.dma_start(offs_t[:], offs)
+
+        xs_first = own([P, T], U8, "xs_first", tag="after_first_bytes")
+        nc.gpsimd.memset(xs_first[:].bitcast(I32), 0)
+        xs_src = x_scales.bitcast(I32).rearrange("s (q r) c -> q s r c", r=4)
+        for q in range(4):
+            queue = nc.gpsimd if q < 2 else nc.scalar
+            queue.dma_start(out=xs_first[32 * q : 32 * q + 4 * PASSES, :].bitcast(I32), in_=xs_src[q])
+
+        half = E // 2
+        was = [own([P, half * PASSES, H], U8, f"was{g}") for g in range(2)]
+        was_src = wa_scales.bitcast(I32).rearrange("(g e) s (q r) c -> g r q (e s) c", g=2, r=4)
+        nc.vector.memset(was[0][:].bitcast(I32), 0)
+        for r in range(4):
+            nc.scalar.dma_start(out=was[0][r:P:32, :, :].bitcast(I32), in_=was_src[0, r])
+
+        xw_src = x_words.rearrange("s p t d -> p s (t d)").bitcast(I32)
+        x0 = own([P, T], I32, "x0")
+        nc.sync.dma_start(out=x0[:], in_=xw_src[:, 0, :])
+        x12 = own([P, PASSES - 1, T], I32, "x12")
+        nc.sync.dma_start(out=x12[:], in_=xw_src[:, 1:, :])
+        windows = [x0[:].bitcast(U32)] + [x12[:, s, :].bitcast(U32) for s in range(PASSES - 1)]
+
+        ident = own([P, P], F32, "ident")
+        make_identity(nc, ident[:])
+
+        ws = own([P, E * PASSES, N], U8, "ws")
+        nc.gpsimd.memset(ws[:].bitcast(I32), 0)
+        nc.vector.memset(was[1][:].bitcast(I32), 0)
+        xs_rest = own([P, 2 * T], U8, "xs_rest")
+        nc.vector.memset(xs_rest[:, T:].bitcast(I32), 0)
+        shifted = []
+        for g, (e0, e1) in enumerate(BYTE_GROUPS):
+            sh = own([P, PASSES - 1, (e1 - e0) * C], U8, f"shifted{g}")
+            nc.gpsimd.memset(sh[:].bitcast(I32), 0)
+            shifted.append(sh)
+
+        wa_src = wa_words.rearrange("e s p i d -> e p s (i d)").bitcast(I32)
+        w_src = w_words.bitcast(I32).rearrange("(g e) s p c -> g p (e s) c", e=2)
+        wb_src = wb.rearrange("(g e) (p j) n -> g p e (j n)", e=2, j=4)
+        wa_t, w_t, wb_raw = {}, {}, {}
+
+        def load_wa(e):
+            wa_t[e] = held.tile([P, PASSES, H], I32, name=f"wa{e}", tag="wa", bufs=3, align_bytes=64)
+            nc.sync.dma_start(out=wa_t[e][:], in_=wa_src[e])
+
+        def load_pair(g):
+            wb_raw[g] = ring.tile([P, 2, 4 * N], F32, name=f"wb_raw{g}", tag="wb_raw")
+            nc.sync.dma_start(out=wb_raw[g][:], in_=wb_src[g])
+            w_t[g] = ring.tile([P, 2 * PASSES, 2 * N], U8, name=f"w{g}", tag="w", align_bytes=64)
+            nc.sync.dma_start(out=w_t[g][:].bitcast(I32), in_=w_src[g])
+
+        load_wa(0)
+        load_wa(1)
+        load_pair(0)
+        ws_src = w_scales.bitcast(I32).rearrange("e s (q r) c -> r q (e s) c", r=4)
+        for r in range(4):
+            nc.sync.dma_start(out=ws[r:P:32, :, :].bitcast(I32), in_=ws_src[r])
+        load_wa(2)
+        for r in range(4):
+            nc.sync.dma_start(out=was[1][r:P:32, :, :].bitcast(I32), in_=was_src[1, r])
+        load_pair(1)
+        pos_t = []
+        for r, pos in enumerate((pos1, pos2, pos3)):
+            tile = held.tile([P, T // 16], U16, name=f"pos_t{r}")
+            nc.sync.dma_start(tile[:], pos)
+            pos_t.append(tile)
+
+        y_all = own([P, SLOTS], F32, "y_all")
+        planes, xg, hb, wq = {}, {}, {}, {}
+
+        def spans(e):
+            return ((0, P), (P, C)) if e == E - 1 else ((0, C),)
+
+        def offsets(first, last):
+            return offs_t[:, first // 16 : last // 16]
+
+        def gather_bytes(g):
+            e0, e1 = BYTE_GROUPS[g]
+            tile = own([P, (e1 - e0) * C], U8, f"planes{g}")
+            window = xs_first[:] if g == 0 else xs_rest[:]
+            nc.vector.tensor_copy(tile[:], window.indirect(offsets(e0 * C, e1 * C)))
+            if g == 0:
+                nc.vector.tensor_copy(xs_rest[:, :T].bitcast(I32), xs_first[:].bitcast(I32))
+            for s in range(1, PASSES):
+                nc.gpsimd.dma_start(
+                    out=shifted[g][0:SHIFT_ROWS, s - 1, :].bitcast(I32),
+                    in_=tile[4 * s : 4 * s + SHIFT_ROWS, :].bitcast(I32),
+                )
+            for e in range(e0, e1):
+                planes[e] = (tile, shifted[g], (e - e0) * C)
+
+        def gather_words(e, tile):
+            xg[e] = tile
+            for a, b in spans(e):
+                for s in range(PASSES):
+                    nc.vector.tensor_copy(tile[:, s, a:b], windows[s].indirect(offsets(e * C + a, e * C + b)))
+
+        def quantise_wb(g):
+            grouped = ring.tile([P, 2, N * 4], BF16, name=f"wb_bf{g}", tag="wb_bf", align_bytes=64)
+            for e in range(2):
+                nc.scalar.copy(
+                    out=grouped[:, e, :].rearrange("p (c i j) -> p c j i", i=4, j=4),
+                    in_=wb_raw[g][:, e, :].rearrange("p (j c i) -> p c j i", i=4, j=4),
+                )
+            codes = own([P, 2 * N], U32, f"wb_codes{g}")
+            scales = own([P, 2 * N], U8, f"wb_scales{g}")
+            nc.vector.quantize_mx(
+                out=codes[:].bitcast(FP8X4), scales=scales[:], in_=grouped[:].rearrange("p e c -> p (e c)")
+            )
+            wq[g] = (codes, scales)
+
+        def hidden(e):
+            tile, shift, c0 = planes[e]
+            h_rows = []
+            for b in range(2):
+                row = ring.tile([P, H], BF16, name=f"h_rows{e}_{b}", tag=f"h_rows{b}")
+                h_rows.append(row)
+                acc = psum.tile([P, H], F32, name=f"h{e}_{b}", tag=f"h{b}{e % 2}")
+                for s in range(PASSES):
+                    nc.tensor.matmul_mx(
+                        out=acc[:],
+                        lhsT=xg[e][:, s, b * P : (b + 1) * P].bitcast(FP8X4),
+                        lhsT_scale=tile[4 * s :, c0 + b * P : c0 + (b + 1) * P],
+                        rhs=wa_t[e][:, s, :].bitcast(FP8X4),
+                        rhs_scale=was[e // half][:, (e % half) * PASSES + s, :],
+                        start=(s == 0),
+                        stop=(s == PASSES - 1),
+                    )
+                nc.scalar.activation(
+                    out=row[:].rearrange("p (u m d) -> p u m d", u=2, d=2),
+                    in_=acc[:].rearrange("p (m u d) -> p u m d", u=2, d=2),
+                    func=SILU,
+                )
+            return h_rows
+
+        def turn(e, h_rows):
+            for a, b in spans(e):
+                blocks = range(a // P, b // P)
+                turned = psum.tile([P, len(blocks), 2, P], F32, name=f"t{e}_{a}", tag=f"t{(e + a // P) % 2}")
+                for k, blk in enumerate(blocks):
+                    for u in range(2):
+                        nc.tensor.transpose(turned[:, k, u, :], h_rows[blk][:].bitcast(F32)[:, u * P : (u + 1) * P], ident[:])
+                grouped = own([P, 4 * (b - a)], BF16, f"hb{e}_{a}", tag=f"link{e}_{a}")
+                nc.scalar.copy(
+                    out=grouped[:].bitcast(F32).rearrange("p (k j u) -> p k j u", u=2, j=P),
+                    in_=turned[:].rearrange("p k u j -> p k j u"),
+                )
+                hb[e, a] = grouped
+
+        def second(e):
+            tile, shift, c0 = planes[e]
+            wcodes, wscales = wq[e // 2]
+            wcols = slice((e % 2) * N, (e % 2 + 1) * N)
+            for a, b in spans(e):
+                codes = ring.tile([P, b - a], U32, name=f"hq{e}_{a}", tag="hq", align_bytes=64)
+                scales = ring.tile([P, b - a], U8, name=f"hs{e}_{a}", tag="hs", align_bytes=64)
+                nc.vector.quantize_mx(out=codes[:].bitcast(FP8X4), scales=scales[:], in_=hb[e, a][:])
+                tag = f"t{(e + a // P) % 2}" if e == E - 1 else f"h0{e % 2}"
+                acc = psum.tile([P, b - a], F32, name=f"y{e}_{a}", tag=tag)
+                for c in range(a, b, P):
+                    for s in range(PASSES):
+                        cols = slice(c0 + c, c0 + c + P)
+                        nc.tensor.matmul_mx(
+                            out=acc[:, c - a : c - a + P],
+                            lhsT=w_t[e // 2][:, (e % 2) * PASSES + s, :].bitcast(FP4X4),
+                            lhsT_scale=ws[:, e * PASSES + s, :],
+                            rhs=xg[e][:, s, c : c + P].bitcast(FP8X4),
+                            rhs_scale=tile[:, cols] if s == 0 else shift[:, s - 1, cols],
+                            start=(s == 0),
+                            stop=False,
+                        )
+                    nc.tensor.matmul_mx(
+                        out=acc[:, c - a : c - a + P],
+                        lhsT=wcodes[:, wcols].bitcast(FP8X4),
+                        lhsT_scale=wscales[:, wcols],
+                        rhs=codes[:, c - a : c - a + P].bitcast(FP8X4),
+                        rhs_scale=scales[:, c - a : c - a + P],
+                        start=False,
+                        stop=True,
+                    )
+                nc.scalar.copy(out=y_all[:, e * C + a : e * C + b], in_=acc[:])
+
+        gather_words(0, own([P, PASSES, C], U32, "xg0"))
+        gather_bytes(0)
+        gather_bytes(1)
+        early = own([P, LAG - 1, PASSES, C], U32, "xg_early", tag="after_first_bytes")
+        rows = {}
+        for e in range(E):
+            if 1 <= e < LAG:
+                gather_words(e, early[:, e - 1, :, :])
+            if e == LAG:
+                gather_bytes(2)
+            if e >= LAG:
+                load_wa(e)
+                gather_words(e, own([P, PASSES, C], U32, f"xg{e}", tag=f"link{e - LAG}_0"))
+            rows[e] = hidden(e)
+            if e >= 1:
+                turn(e - 1, rows[e - 1])
+            if e % 2 == 0:
+                quantise_wb(e // 2)
+            if e == 2:
+                load_pair(2)
+            if e >= LAG - 1:
+                second(e - (LAG - 1))
+        gate_t = held.tile([P, TOP, T], F32, name="gate_t", tag="wa", bufs=3, align_bytes=64)
+        nc.sync.dma_start(out=gate_t[:], in_=gate.rearrange("r p t -> p r t"))
+        turn(E - 1, rows[E - 1])
+        for e in range(E - LAG + 1, E):
+            second(e)
+
+        width = T // 2
+        prods, sums = {}, {}
+        for part in range(2):
+            cols = slice(part * width, (part + 1) * width)
+            for r in range(TOP):
+                prods[part, r] = own([P, width], F32, f"prod{part}_{r}")
+                nc.vector.tensor_tensor(
+                    prods[part, r][:],
+                    y_all[:].indirect(pos_t[r][:, part * width // 16 : (part + 1) * width // 16]),
+                    gate_t[:, r, cols],
+                    MULT,
+                )
+            pair = own([P, width], F32, f"pair{part}")
+            nc.vector.tensor_tensor(pair[:], prods[part, 0][:], prods[part, 1][:], ADD)
+            total = own([P, width], F32, f"total{part}")
+            nc.vector.tensor_tensor(total[:], pair[:], prods[part, 2][:], ADD)
+            nc.sync.dma_start(out=out[:, cols], in_=total[:])

@@ -23,7 +23,9 @@ ADD = mybir.AluOpType.add
 
 BYTE_GROUPS = ((0, 1), (1, 3), (3, 6))
 LAG = 3
-SHIFT_ROWS = 112
+PLANE_ROWS = 100
+WA_BUFS = 3
+HALF = E // 2
 
 
 def tile_moe_elr_silu_kernel(
@@ -48,33 +50,31 @@ def tile_moe_elr_silu_kernel(
             queue = nc.gpsimd if q < 2 else nc.scalar
             queue.dma_start(out=xs_first[32 * q : 32 * q + 4 * PASSES, :].bitcast(I32), in_=xs_src[q])
 
-        half = E // 2
-        was = [own([P, half * PASSES, H], U8, f"was{g}") for g in range(2)]
+        wa_planes = [own([P, HALF * PASSES, H], U8, f"was{part}") for part in range(2)]
         was_src = wa_scales.bitcast(I32).rearrange("(g e) s (q r) c -> g r q (e s) c", g=2, r=4)
-        nc.vector.memset(was[0][:].bitcast(I32), 0)
+        nc.vector.memset(wa_planes[0][:].bitcast(I32), 0)
         for r in range(4):
-            nc.scalar.dma_start(out=was[0][r:P:32, :, :].bitcast(I32), in_=was_src[0, r])
+            nc.scalar.dma_start(out=wa_planes[0][r:P:32, :, :].bitcast(I32), in_=was_src[0, r])
 
         xw_src = x_words.rearrange("s p t d -> p s (t d)").bitcast(I32)
         x0 = own([P, T], I32, "x0")
         nc.sync.dma_start(out=x0[:], in_=xw_src[:, 0, :])
         x12 = own([P, PASSES - 1, T], I32, "x12")
         nc.sync.dma_start(out=x12[:], in_=xw_src[:, 1:, :])
-        windows = [x0[:].bitcast(U32)] + [x12[:, s, :].bitcast(U32) for s in range(PASSES - 1)]
+        word_windows = [x0[:].bitcast(U32)] + [x12[:, s, :].bitcast(U32) for s in range(PASSES - 1)]
 
         ident = own([P, P], F32, "ident")
         make_identity(nc, ident[:])
 
-        ws = own([P, E * PASSES, N], U8, "ws")
-        nc.gpsimd.memset(ws[:].bitcast(I32), 0)
-        nc.vector.memset(was[1][:].bitcast(I32), 0)
+        w_planes = own([P, E * PASSES, N], U8, "ws")
+        nc.gpsimd.memset(w_planes[:].bitcast(I32), 0)
+        nc.vector.memset(wa_planes[1][:].bitcast(I32), 0)
         xs_rest = own([P, 2 * T], U8, "xs_rest")
         nc.vector.memset(xs_rest[:, T:].bitcast(I32), 0)
         shifted = []
-        for g, (e0, e1) in enumerate(BYTE_GROUPS):
-            sh = own([P, PASSES - 1, (e1 - e0) * C], U8, f"shifted{g}")
-            nc.gpsimd.memset(sh[:].bitcast(I32), 0)
-            shifted.append(sh)
+        for group, (e0, e1) in enumerate(BYTE_GROUPS):
+            shifted.append(own([P, PASSES - 1, (e1 - e0) * C], U8, f"shifted{group}"))
+            nc.gpsimd.memset(shifted[group][:].bitcast(I32), 0)
 
         wa_src = wa_words.rearrange("e s p i d -> e p s (i d)").bitcast(I32)
         w_src = w_words.bitcast(I32).rearrange("(g e) s p c -> g p (e s) c", e=2)
@@ -82,33 +82,32 @@ def tile_moe_elr_silu_kernel(
         wa_t, w_t, wb_raw = {}, {}, {}
 
         def load_wa(e):
-            wa_t[e] = held.tile([P, PASSES, H], I32, name=f"wa{e}", tag="wa", bufs=3, align_bytes=64)
+            wa_t[e] = held.tile([P, PASSES, H], I32, name=f"wa{e}", tag="wa", bufs=WA_BUFS, align_bytes=64)
             nc.sync.dma_start(out=wa_t[e][:], in_=wa_src[e])
 
-        def load_pair(g):
-            wb_raw[g] = ring.tile([P, 2, 4 * N], F32, name=f"wb_raw{g}", tag="wb_raw")
-            nc.sync.dma_start(out=wb_raw[g][:], in_=wb_src[g])
-            w_t[g] = ring.tile([P, 2 * PASSES, 2 * N], U8, name=f"w{g}", tag="w", align_bytes=64)
-            nc.sync.dma_start(out=w_t[g][:].bitcast(I32), in_=w_src[g])
+        def load_pair(pair):
+            wb_raw[pair] = ring.tile([P, 2, 4 * N], F32, name=f"wb_raw{pair}", tag="wb_raw")
+            nc.sync.dma_start(out=wb_raw[pair][:], in_=wb_src[pair])
+            w_t[pair] = ring.tile([P, 2 * PASSES, 2 * N], U8, name=f"w{pair}", tag="w", align_bytes=64)
+            nc.sync.dma_start(out=w_t[pair][:].bitcast(I32), in_=w_src[pair])
 
         load_wa(0)
         load_wa(1)
         load_pair(0)
         ws_src = w_scales.bitcast(I32).rearrange("e s (q r) c -> r q (e s) c", r=4)
         for r in range(4):
-            nc.sync.dma_start(out=ws[r:P:32, :, :].bitcast(I32), in_=ws_src[r])
+            nc.sync.dma_start(out=w_planes[r:P:32, :, :].bitcast(I32), in_=ws_src[r])
         load_wa(2)
         for r in range(4):
-            nc.sync.dma_start(out=was[1][r:P:32, :, :].bitcast(I32), in_=was_src[1, r])
+            nc.sync.dma_start(out=wa_planes[1][r:P:32, :, :].bitcast(I32), in_=was_src[1, r])
         load_pair(1)
         pos_t = []
-        for r, pos in enumerate((pos1, pos2, pos3)):
-            tile = held.tile([P, T // 16], U16, name=f"pos_t{r}")
-            nc.sync.dma_start(tile[:], pos)
-            pos_t.append(tile)
+        for choice, pos in enumerate((pos1, pos2, pos3)):
+            pos_t.append(held.tile([P, T // 16], U16, name=f"pos_t{choice}"))
+            nc.sync.dma_start(pos_t[choice][:], pos)
 
         y_all = own([P, SLOTS], F32, "y_all")
-        planes, xg, hb, wq = {}, {}, {}, {}
+        slot_planes, slot_words, h_grouped, wb_quantised = {}, {}, {}, {}
 
         def spans(e):
             return ((0, P), (P, C)) if e == E - 1 else ((0, C),)
@@ -116,61 +115,60 @@ def tile_moe_elr_silu_kernel(
         def offsets(first, last):
             return offs_t[:, first // 16 : last // 16]
 
-        def gather_bytes(g):
-            e0, e1 = BYTE_GROUPS[g]
-            tile = own([P, (e1 - e0) * C], U8, f"planes{g}")
-            window = xs_first[:] if g == 0 else xs_rest[:]
-            nc.vector.tensor_copy(tile[:], window.indirect(offsets(e0 * C, e1 * C)))
-            if g == 0:
+        def gather_bytes(group):
+            e0, e1 = BYTE_GROUPS[group]
+            gathered = own([P, (e1 - e0) * C], U8, f"planes{group}")
+            window = xs_first[:] if group == 0 else xs_rest[:]
+            nc.vector.tensor_copy(gathered[:], window.indirect(offsets(e0 * C, e1 * C)))
+            if group == 0:
                 nc.vector.tensor_copy(xs_rest[:, :T].bitcast(I32), xs_first[:].bitcast(I32))
             for s in range(1, PASSES):
                 nc.gpsimd.dma_start(
-                    out=shifted[g][0:SHIFT_ROWS, s - 1, :].bitcast(I32),
-                    in_=tile[4 * s : 4 * s + SHIFT_ROWS, :].bitcast(I32),
+                    out=shifted[group][0:PLANE_ROWS, s - 1, :].bitcast(I32),
+                    in_=gathered[4 * s : 4 * s + PLANE_ROWS, :].bitcast(I32),
                 )
             for e in range(e0, e1):
-                planes[e] = (tile, shifted[g], (e - e0) * C)
+                slot_planes[e] = (gathered, shifted[group], (e - e0) * C)
 
-        def gather_words(e, tile):
-            xg[e] = tile
+        def gather_words(e, words):
+            slot_words[e] = words
             for a, b in spans(e):
                 for s in range(PASSES):
-                    nc.vector.tensor_copy(tile[:, s, a:b], windows[s].indirect(offsets(e * C + a, e * C + b)))
+                    nc.vector.tensor_copy(words[:, s, a:b], word_windows[s].indirect(offsets(e * C + a, e * C + b)))
 
-        def quantise_wb(g):
-            grouped = ring.tile([P, 2, N * 4], BF16, name=f"wb_bf{g}", tag="wb_bf", align_bytes=64)
-            for e in range(2):
+        def quantise_wb(pair):
+            wb_grouped = ring.tile([P, 2, N * 4], BF16, name=f"wb_bf{pair}", tag="wb_bf", align_bytes=64)
+            for member in range(2):
                 nc.scalar.copy(
-                    out=grouped[:, e, :].rearrange("p (c i j) -> p c j i", i=4, j=4),
-                    in_=wb_raw[g][:, e, :].rearrange("p (j c i) -> p c j i", i=4, j=4),
+                    out=wb_grouped[:, member, :].rearrange("p (c m j) -> p c j m", m=4, j=4),
+                    in_=wb_raw[pair][:, member, :].rearrange("p (j c m) -> p c j m", m=4, j=4),
                 )
-            codes = own([P, 2 * N], U32, f"wb_codes{g}")
-            scales = own([P, 2 * N], U8, f"wb_scales{g}")
+            wb_codes = own([P, 2 * N], U32, f"wb_codes{pair}")
+            wb_plane = own([P, 2 * N], U8, f"wb_scales{pair}")
             nc.vector.quantize_mx(
-                out=codes[:].bitcast(FP8X4), scales=scales[:], in_=grouped[:].rearrange("p e c -> p (e c)")
+                out=wb_codes[:].bitcast(FP8X4), scales=wb_plane[:], in_=wb_grouped[:].rearrange("p e c -> p (e c)")
             )
-            wq[g] = (codes, scales)
+            wb_quantised[pair] = (wb_codes, wb_plane)
 
         def hidden(e):
-            tile, shift, c0 = planes[e]
+            gathered, first = slot_planes[e][0], slot_planes[e][2]
             h_rows = []
-            for b in range(2):
-                row = ring.tile([P, H], BF16, name=f"h_rows{e}_{b}", tag=f"h_rows{b}")
-                h_rows.append(row)
-                acc = psum.tile([P, H], F32, name=f"h{e}_{b}", tag=f"h{b}{e % 2}")
+            for block in range(2):
+                h_rows.append(ring.tile([P, H], BF16, name=f"h_rows{e}_{block}", tag=f"h_rows{block}"))
+                h_sum = psum.tile([P, H], F32, name=f"h{e}_{block}", tag=f"h{block}{e % 2}")
                 for s in range(PASSES):
                     nc.tensor.matmul_mx(
-                        out=acc[:],
-                        lhsT=xg[e][:, s, b * P : (b + 1) * P].bitcast(FP8X4),
-                        lhsT_scale=tile[4 * s :, c0 + b * P : c0 + (b + 1) * P],
+                        out=h_sum[:],
+                        lhsT=slot_words[e][:, s, block * P : (block + 1) * P].bitcast(FP8X4),
+                        lhsT_scale=gathered[4 * s :, first + block * P : first + (block + 1) * P],
                         rhs=wa_t[e][:, s, :].bitcast(FP8X4),
-                        rhs_scale=was[e // half][:, (e % half) * PASSES + s, :],
+                        rhs_scale=wa_planes[e // HALF][:, (e % HALF) * PASSES + s, :],
                         start=(s == 0),
                         stop=(s == PASSES - 1),
                     )
                 nc.scalar.activation(
-                    out=row[:].rearrange("p (u m d) -> p u m d", u=2, d=2),
-                    in_=acc[:].rearrange("p (m u d) -> p u m d", u=2, d=2),
+                    out=h_rows[block][:].rearrange("p (v m d) -> p v m d", v=2, d=2),
+                    in_=h_sum[:].rearrange("p (m v d) -> p v m d", v=2, d=2),
                     func=SILU,
                 )
             return h_rows
@@ -179,58 +177,58 @@ def tile_moe_elr_silu_kernel(
             for a, b in spans(e):
                 blocks = range(a // P, b // P)
                 turned = psum.tile([P, len(blocks), 2, P], F32, name=f"t{e}_{a}", tag=f"t{(e + a // P) % 2}")
-                for k, blk in enumerate(blocks):
-                    for u in range(2):
-                        nc.tensor.transpose(turned[:, k, u, :], h_rows[blk][:].bitcast(F32)[:, u * P : (u + 1) * P], ident[:])
-                grouped = own([P, 4 * (b - a)], BF16, f"hb{e}_{a}", tag=f"link{e}_{a}")
+                for place, block in enumerate(blocks):
+                    for v in range(2):
+                        half_row = h_rows[block][:].bitcast(F32)[:, v * P : (v + 1) * P]
+                        nc.tensor.transpose(turned[:, place, v, :], half_row, ident[:])
+                h_grouped[e, a] = own([P, 4 * (b - a)], BF16, f"hb{e}_{a}", tag=f"link{e}_{a}")
                 nc.scalar.copy(
-                    out=grouped[:].bitcast(F32).rearrange("p (k j u) -> p k j u", u=2, j=P),
-                    in_=turned[:].rearrange("p k u j -> p k j u"),
+                    out=h_grouped[e, a][:].bitcast(F32).rearrange("p (g j v) -> p g j v", v=2, j=P),
+                    in_=turned[:].rearrange("p g v j -> p g j v"),
                 )
-                hb[e, a] = grouped
 
-        def second(e):
-            tile, shift, c0 = planes[e]
-            wcodes, wscales = wq[e // 2]
-            wcols = slice((e % 2) * N, (e % 2 + 1) * N)
+        def results(e):
+            gathered, moved, first = slot_planes[e]
+            wb_codes, wb_plane = wb_quantised[e // 2]
+            wb_cols = slice((e % 2) * N, (e % 2 + 1) * N)
             for a, b in spans(e):
-                codes = ring.tile([P, b - a], U32, name=f"hq{e}_{a}", tag="hq", align_bytes=64)
-                scales = ring.tile([P, b - a], U8, name=f"hs{e}_{a}", tag="hs", align_bytes=64)
-                nc.vector.quantize_mx(out=codes[:].bitcast(FP8X4), scales=scales[:], in_=hb[e, a][:])
-                tag = f"t{(e + a // P) % 2}" if e == E - 1 else f"h0{e % 2}"
-                acc = psum.tile([P, b - a], F32, name=f"y{e}_{a}", tag=tag)
+                h_codes = ring.tile([P, b - a], U32, name=f"hq{e}_{a}", tag="hq", align_bytes=64)
+                h_plane = ring.tile([P, b - a], U8, name=f"hs{e}_{a}", tag="hs", align_bytes=64)
+                nc.vector.quantize_mx(out=h_codes[:].bitcast(FP8X4), scales=h_plane[:], in_=h_grouped[e, a][:])
+                bank = f"t{(e + a // P) % 2}" if e == E - 1 else f"h0{e % 2}"
+                y_sum = psum.tile([P, b - a], F32, name=f"y{e}_{a}", tag=bank)
                 for c in range(a, b, P):
                     for s in range(PASSES):
-                        cols = slice(c0 + c, c0 + c + P)
+                        plane_cols = slice(first + c, first + c + P)
                         nc.tensor.matmul_mx(
-                            out=acc[:, c - a : c - a + P],
+                            out=y_sum[:, c - a : c - a + P],
                             lhsT=w_t[e // 2][:, (e % 2) * PASSES + s, :].bitcast(FP4X4),
-                            lhsT_scale=ws[:, e * PASSES + s, :],
-                            rhs=xg[e][:, s, c : c + P].bitcast(FP8X4),
-                            rhs_scale=tile[:, cols] if s == 0 else shift[:, s - 1, cols],
+                            lhsT_scale=w_planes[:, e * PASSES + s, :],
+                            rhs=slot_words[e][:, s, c : c + P].bitcast(FP8X4),
+                            rhs_scale=gathered[:, plane_cols] if s == 0 else moved[:, s - 1, plane_cols],
                             start=(s == 0),
                             stop=False,
                         )
                     nc.tensor.matmul_mx(
-                        out=acc[:, c - a : c - a + P],
-                        lhsT=wcodes[:, wcols].bitcast(FP8X4),
-                        lhsT_scale=wscales[:, wcols],
-                        rhs=codes[:, c - a : c - a + P].bitcast(FP8X4),
-                        rhs_scale=scales[:, c - a : c - a + P],
+                        out=y_sum[:, c - a : c - a + P],
+                        lhsT=wb_codes[:, wb_cols].bitcast(FP8X4),
+                        lhsT_scale=wb_plane[:, wb_cols],
+                        rhs=h_codes[:, c - a : c - a + P].bitcast(FP8X4),
+                        rhs_scale=h_plane[:, c - a : c - a + P],
                         start=False,
                         stop=True,
                     )
-                nc.scalar.copy(out=y_all[:, e * C + a : e * C + b], in_=acc[:])
+                nc.scalar.copy(out=y_all[:, e * C + a : e * C + b], in_=y_sum[:])
 
         gather_words(0, own([P, PASSES, C], U32, "xg0"))
         gather_bytes(0)
         gather_bytes(1)
-        early = own([P, LAG - 1, PASSES, C], U32, "xg_early", tag="after_first_bytes")
+        early_words = own([P, LAG - 1, PASSES, C], U32, "xg_early", tag="after_first_bytes")
         rows = {}
         for e in range(E):
             if 1 <= e < LAG:
-                gather_words(e, early[:, e - 1, :, :])
-            if e == LAG:
+                gather_words(e, early_words[:, e - 1, :, :])
+            if e == BYTE_GROUPS[2][0]:
                 gather_bytes(2)
             if e >= LAG:
                 load_wa(e)
@@ -243,27 +241,27 @@ def tile_moe_elr_silu_kernel(
             if e == 2:
                 load_pair(2)
             if e >= LAG - 1:
-                second(e - (LAG - 1))
-        gate_t = held.tile([P, TOP, T], F32, name="gate_t", tag="wa", bufs=3, align_bytes=64)
+                results(e - (LAG - 1))
+        gate_t = held.tile([P, TOP, T], F32, name="gate_t", tag="wa", bufs=WA_BUFS, align_bytes=64)
         nc.sync.dma_start(out=gate_t[:], in_=gate.rearrange("r p t -> p r t"))
         turn(E - 1, rows[E - 1])
         for e in range(E - LAG + 1, E):
-            second(e)
+            results(e)
 
         width = T // 2
-        prods, sums = {}, {}
         for part in range(2):
-            cols = slice(part * width, (part + 1) * width)
-            for r in range(TOP):
-                prods[part, r] = own([P, width], F32, f"prod{part}_{r}")
+            tokens = slice(part * width, (part + 1) * width)
+            weighted = []
+            for choice in range(TOP):
+                weighted.append(own([P, width], F32, f"prod{part}_{choice}"))
                 nc.vector.tensor_tensor(
-                    prods[part, r][:],
-                    y_all[:].indirect(pos_t[r][:, part * width // 16 : (part + 1) * width // 16]),
-                    gate_t[:, r, cols],
+                    weighted[choice][:],
+                    y_all[:].indirect(pos_t[choice][:, part * width // 16 : (part + 1) * width // 16]),
+                    gate_t[:, choice, tokens],
                     MULT,
                 )
-            pair = own([P, width], F32, f"pair{part}")
-            nc.vector.tensor_tensor(pair[:], prods[part, 0][:], prods[part, 1][:], ADD)
+            two = own([P, width], F32, f"pair{part}")
+            nc.vector.tensor_tensor(two[:], weighted[0][:], weighted[1][:], ADD)
             total = own([P, width], F32, f"total{part}")
-            nc.vector.tensor_tensor(total[:], pair[:], prods[part, 2][:], ADD)
-            nc.sync.dma_start(out=out[:, cols], in_=total[:])
+            nc.vector.tensor_tensor(total[:], two[:], weighted[2][:], ADD)
+            nc.sync.dma_start(out=out[:, tokens], in_=total[:])

@@ -21,11 +21,8 @@ SILU = mybir.ActivationFunctionType.Silu
 MULT = mybir.AluOpType.mult
 ADD = mybir.AluOpType.add
 
-BYTE_GROUPS = ((0, 1), (1, 3), (3, 6))
-LAG = 3
 PLANE_ROWS = 100
-WA_BUFS = 3
-HALF = E // 2
+DENSE = 8
 
 
 def tile_moe_elr_silu_kernel(
@@ -34,114 +31,179 @@ def tile_moe_elr_silu_kernel(
     nc = tc.nc
     with ExitStack() as ctx:
         held = ctx.enter_context(tc.tile_pool(name="held", bufs=1))
-        ring = ctx.enter_context(tc.tile_pool(name="ring", bufs=2))
         psum = ctx.enter_context(tc.psum_pool(name="psum", bufs=1))
 
         def own(shape, dtype, name, tag=None):
             return held.tile(shape, dtype, name=name, tag=tag or name, align_bytes=64)
 
+        xs_first = own([P, T], U8, "xs_first")
+        nc.gpsimd.memset(xs_first[:].bitcast(I32), 0)
         offs_t = held.tile([P, SLOTS // 16], U16, name="offs_t")
         nc.sync.dma_start(offs_t[:], offs)
 
-        xs_first = own([P, T], U8, "xs_first", tag="after_first_bytes")
-        nc.gpsimd.memset(xs_first[:].bitcast(I32), 0)
+        was_src = wa_scales.bitcast(I32).rearrange("e s (q r) c -> q (e s) r c", r=4)
+        wa_src = wa_words.rearrange("e s p i d -> e p s (i d)").bitcast(I32)
+        xw_src = x_words.rearrange("s p t d -> p s (t d)").bitcast(I32)
         xs_src = x_scales.bitcast(I32).rearrange("s (q r) c -> q s r c", r=4)
-        for q in range(4):
-            queue = nc.gpsimd if q < 2 else nc.scalar
+        wa_t = {}
+
+        def load_dense(plane, group, q):
+            rows = was_src[q, DENSE * group : min(DENSE * (group + 1), E * PASSES)]
+            nc.sync.dma_start(out=plane[32 * q : 32 * q + 4 * rows.shape[0], :].bitcast(I32), in_=rows)
+
+        def load_wa(e, words):
+            nc.sync.dma_start(out=words.rearrange("p (s c) -> p s c", s=PASSES), in_=wa_src[e])
+            for s in range(PASSES):
+                wa_t[e, s] = words[:, s * H : (s + 1) * H]
+
+        def move_up(queue, group, rows):
+            queue.dma_start(
+                out=raised[group, rows][0 : P - rows, :].bitcast(I32), in_=dense[group][rows:P, :].bitcast(I32)
+            )
+
+        def load_xs(queue, q):
             queue.dma_start(out=xs_first[32 * q : 32 * q + 4 * PASSES, :].bitcast(I32), in_=xs_src[q])
 
-        wa_planes = [own([P, HALF * PASSES, H], U8, f"was{part}") for part in range(2)]
-        was_src = wa_scales.bitcast(I32).rearrange("(g e) s (q r) c -> g r q (e s) c", g=2, r=4)
-        nc.vector.memset(wa_planes[0][:].bitcast(I32), 0)
-        for r in range(4):
-            nc.scalar.dma_start(out=wa_planes[0][r:P:32, :, :].bitcast(I32), in_=was_src[0, r])
+        w_src = w_words.bitcast(I32).rearrange("e s p c -> p (e s) c")
+        wb_src = wb.rearrange("(g e) (p j) n -> g p e (j n)", e=2, j=4)
+        ws_src = w_scales.bitcast(I32).rearrange("e s (q r) c -> r q (e s) c", r=4)
+        w_t, wb_raw, gate_t, late, pos_t = {}, {}, [], {}, []
 
-        xw_src = x_words.rearrange("s p t d -> p s (t d)").bitcast(I32)
-        x0 = own([P, T], I32, "x0")
-        nc.sync.dma_start(out=x0[:], in_=xw_src[:, 0, :])
-        x12 = own([P, PASSES - 1, T], I32, "x12")
-        nc.sync.dma_start(out=x12[:], in_=xw_src[:, 1:, :])
-        word_windows = [x0[:].bitcast(U32)] + [x12[:, s, :].bitcast(U32) for s in range(PASSES - 1)]
+        def load_wb(pair, tag):
+            wb_raw[pair] = own([P, 2, 4 * N], F32, f"wb_raw{pair}", tag=tag)[:]
+            nc.sync.dma_start(out=wb_raw[pair], in_=wb_src[pair])
+
+        def load_w(e0, e1, tag):
+            words = own([P, (e1 - e0) * PASSES, 2 * N], U8, f"w{e0}", tag=tag)
+            nc.sync.dma_start(out=words[:].bitcast(I32), in_=w_src[:, e0 * PASSES : e1 * PASSES, :])
+            for e in range(e0, e1):
+                w_t[e] = words[:, (e - e0) * PASSES : (e - e0 + 1) * PASSES, :]
+
+        for q in range(4):
+            load_xs(nc.gpsimd if q < 2 else nc.scalar, q)
+        dense = [own([P, H], U8, "dense0")[:]]
+        load_dense(dense[0], 0, 0)
+        x_rest = own([P, PASSES, T], I32, "x_rest")
+        nc.sync.dma_start(out=x_rest[:, 0:2, :], in_=xw_src[:, 0:2, :])
+        load_dense(dense[0], 0, 1)
+        x_last = own([P, T], I32, "x_last")
+        nc.sync.dma_start(out=x_last[:], in_=xw_src[:, 2, :])
+        load_wa(0, own([P, PASSES * H], I32, "wa0")[:])
+        load_dense(dense[0], 0, 2)
+        load_dense(dense[0], 0, 3)
+        load_wa(1, own([P, PASSES * H], I32, "wa1")[:])
 
         ident = own([P, P], F32, "ident")
         make_identity(nc, ident[:])
-
-        w_planes = own([P, E * PASSES, N], U8, "ws")
-        nc.gpsimd.memset(w_planes[:].bitcast(I32), 0)
-        nc.vector.memset(wa_planes[1][:].bitcast(I32), 0)
-        xs_rest = own([P, 2 * T], U8, "xs_rest")
-        nc.vector.memset(xs_rest[:, T:].bitcast(I32), 0)
-        shifted = []
-        for group, (e0, e1) in enumerate(BYTE_GROUPS):
-            shifted.append(own([P, PASSES - 1, (e1 - e0) * C], U8, f"shifted{group}"))
-            nc.gpsimd.memset(shifted[group][:].bitcast(I32), 0)
-
-        wa_src = wa_words.rearrange("e s p i d -> e p s (i d)").bitcast(I32)
-        w_src = w_words.bitcast(I32).rearrange("(g e) s p c -> g p (e s) c", e=2)
-        wb_src = wb.rearrange("(g e) (p j) n -> g p e (j n)", e=2, j=4)
-        wa_t, w_t, wb_raw = {}, {}, {}
-
-        def load_wa(e):
-            wa_t[e] = held.tile([P, PASSES, H], I32, name=f"wa{e}", tag="wa", bufs=WA_BUFS, align_bytes=64)
-            nc.sync.dma_start(out=wa_t[e][:], in_=wa_src[e])
-
-        def load_pair(pair):
-            wb_raw[pair] = ring.tile([P, 2, 4 * N], F32, name=f"wb_raw{pair}", tag="wb_raw")
-            nc.sync.dma_start(out=wb_raw[pair][:], in_=wb_src[pair])
-            w_t[pair] = ring.tile([P, 2 * PASSES, 2 * N], U8, name=f"w{pair}", tag="w", align_bytes=64)
-            nc.sync.dma_start(out=w_t[pair][:].bitcast(I32), in_=w_src[pair])
-
-        load_wa(0)
-        load_wa(1)
-        load_pair(0)
-        ws_src = w_scales.bitcast(I32).rearrange("e s (q r) c -> r q (e s) c", r=4)
-        for r in range(4):
-            nc.sync.dma_start(out=w_planes[r:P:32, :, :].bitcast(I32), in_=ws_src[r])
-        load_wa(2)
-        for r in range(4):
-            nc.sync.dma_start(out=wa_planes[1][r:P:32, :, :].bitcast(I32), in_=was_src[1, r])
-        load_pair(1)
-        pos_t = []
+        raised = {}
+        for key in ((0, 16), (1, 8), (1, 24)):
+            raised[key] = own([P, H], U8, f"raised{key[0]}_{key[1]}")
+            nc.vector.memset(raised[key][:].bitcast(I32), 0)
+        warm = own([P, 1], F32, "warm")
+        nc.scalar.activation(out=warm[:], in_=raised[1, 8][:, 0:4].bitcast(F32), func=SILU)
+        move_up(nc.scalar, 0, 16)
+        load_wa(2, own([P, PASSES * H], I32, "wa2")[:])
         for choice, pos in enumerate((pos1, pos2, pos3)):
             pos_t.append(held.tile([P, T // 16], U16, name=f"pos_t{choice}"))
             nc.sync.dma_start(pos_t[choice][:], pos)
+        load_w(0, 4, None)
+
+        def wa_plane(e, s):
+            group, place = divmod(e * PASSES + s, DENSE)
+            moved = [rows for g, rows in raised if g == group and rows <= 4 * place]
+            if not moved:
+                return dense[group][4 * place :, :]
+            return raised[group, max(moved)][4 * place - max(moved) :, :]
+
+        shifted = {}
+
+        def shift(part, tag):
+            shifted[part] = own([P, PASSES - 1, SLOTS // 2], U8, f"shifted{part}", tag=tag)
+            nc.gpsimd.memset(shifted[part][:].bitcast(I32), 0)
+            for s in range(1, PASSES):
+                nc.sync.dma_start(
+                    out=shifted[part][0:PLANE_ROWS, s - 1, :].bitcast(I32),
+                    in_=planes[part][4 * s : 4 * s + PLANE_ROWS, :].bitcast(I32),
+                )
+
+        def loads_after_hidden(e):
+            if e == 0:
+                both = own([P, PASSES * H + H // 4], I32, "wa3", tag="wa0")
+                load_wa(3, both[:, : PASSES * H])
+                dense.append(both[:, PASSES * H :].bitcast(U8))
+                for q in range(4):
+                    load_dense(dense[1], 1, q)
+            if e == 1:
+                load_wb(0, "dense0")
+                load_wa(4, own([P, PASSES * H], I32, "wa4", tag="wa1")[:])
+                move_up(nc.sync, 1, 8)
+                move_up(nc.sync, 1, 24)
+            if e == 2:
+                load_wa(5, own([P, PASSES * H], I32, "wa5", tag="wa2")[:])
+
+        def loads_after_turn(e):
+            if e == 0:
+                dense.append(own([P, H], U8, "dense2", tag="h_rows0_0")[:])
+                nc.gpsimd.memset(dense[2].bitcast(I32), 0)
+                for q in range(4):
+                    load_dense(dense[2], 2, q)
+            if e == 1:
+                load_wb(1, "h_rows1_0")
+            if e == 2:
+                late["ws"] = own([P, E * PASSES, N], U8, "ws", tag="h_rows2_0")
+                nc.gpsimd.memset(late["ws"][:].bitcast(I32), 0)
+                load_wb(2, "wa0")
+                for r in range(4):
+                    nc.sync.dma_start(out=late["ws"][r:P:32, :, :].bitcast(I32), in_=ws_src[r])
+                shift(0, "h_rows2_1")
+            if e == 3:
+                load_w(4, 6, "h_rows3_0")
+            if e == 4:
+                shift(1, "wa1")
+                gates = own([P, TOP, T], F32, "gates", tag="h_rows4_0")
+                for choice in range(TOP):
+                    nc.sync.dma_start(out=gates[:, choice, :], in_=gate[choice])
+                    gate_t.append(gates[:, choice, :])
 
         y_all = own([P, SLOTS], F32, "y_all")
-        slot_planes, slot_words, h_grouped, wb_quantised = {}, {}, {}, {}
-
-        def spans(e):
-            return ((0, P), (P, C)) if e == E - 1 else ((0, C),)
+        planes = [own([P, SLOTS // 2], U8, f"planes{part}") for part in range(2)]
+        slot_words, h_grouped, wb_quantised = {}, {}, {}
 
         def offsets(first, last):
             return offs_t[:, first // 16 : last // 16]
 
-        def gather_bytes(group):
-            e0, e1 = BYTE_GROUPS[group]
-            gathered = own([P, (e1 - e0) * C], U8, f"planes{group}")
-            window = xs_first[:] if group == 0 else xs_rest[:]
-            nc.vector.tensor_copy(gathered[:], window.indirect(offsets(e0 * C, e1 * C)))
-            if group == 0:
-                nc.vector.tensor_copy(xs_rest[:, :T].bitcast(I32), xs_first[:].bitcast(I32))
-            for s in range(1, PASSES):
-                nc.gpsimd.dma_start(
-                    out=shifted[group][0:PLANE_ROWS, s - 1, :].bitcast(I32),
-                    in_=gathered[4 * s : 4 * s + PLANE_ROWS, :].bitcast(I32),
+        def gather(e):
+            cols = slice(e % 3 * C, (e % 3 + 1) * C)
+            if e == 0:
+                slot_words[0] = own([P, PASSES, C], U32, "xg0")[:]
+                windows = (x_rest[:, 0, :], x_rest[:, 1, :], x_last[:])
+                nc.vector.tensor_copy(x_rest[:, 2, :], x_last[:])
+            else:
+                slot_words[e] = late["words"][:, e - 1, :, :]
+                windows = [x_rest[:, s, :] for s in range(PASSES)]
+            byte_window = xs_first if e == 0 else late["xs"]
+            nc.vector.tensor_copy(planes[e // 3][:, cols], byte_window[:].indirect(offsets(e * C, (e + 1) * C)))
+            for s in range(PASSES):
+                nc.vector.tensor_copy(
+                    slot_words[e][:, s, :], windows[s].bitcast(U32).indirect(offsets(e * C, (e + 1) * C))
                 )
-            for e in range(e0, e1):
-                slot_planes[e] = (gathered, shifted[group], (e - e0) * C)
-
-        def gather_words(e, words):
-            slot_words[e] = words
-            for a, b in spans(e):
-                for s in range(PASSES):
-                    nc.vector.tensor_copy(words[:, s, a:b], word_windows[s].indirect(offsets(e * C + a, e * C + b)))
+            if e == 0:
+                late["xs"] = own([P, T], U8, "xs_rest", tag="x_last")
+                nc.vector.tensor_copy(late["xs"][:].bitcast(I32), xs_first[:].bitcast(I32))
+                late["words"] = own([P, E - 1, PASSES, C], U32, "xg_late", tag="xs_first")
 
         def quantise_wb(pair):
-            wb_grouped = ring.tile([P, 2, N * 4], BF16, name=f"wb_bf{pair}", tag="wb_bf", align_bytes=64)
-            for member in range(2):
-                nc.scalar.copy(
-                    out=wb_grouped[:, member, :].rearrange("p (c m j) -> p c j m", m=4, j=4),
-                    in_=wb_raw[pair][:, member, :].rearrange("p (j c m) -> p c j m", m=4, j=4),
+            wb_grouped = own([P, 2, N * 4], BF16, f"wb_bf{pair}", tag=("h_rows1_1", "h_rows3_1", None)[pair])
+            if pair < 2:
+                for member in range(2):
+                    nc.scalar.copy(
+                        out=wb_grouped[:, member, :].rearrange("p (c m j) -> p c j m", m=4, j=4),
+                        in_=wb_raw[pair][:, member, :].rearrange("p (j c m) -> p c j m", m=4, j=4),
+                    )
+            else:
+                nc.vector.tensor_copy(
+                    out=wb_grouped[:].rearrange("p e (c m j) -> p e c j m", m=4, j=4),
+                    in_=wb_raw[pair].rearrange("p e (j c m) -> p e c j m", m=4, j=4),
                 )
             wb_codes = own([P, 2 * N], U32, f"wb_codes{pair}")
             wb_plane = own([P, 2 * N], U8, f"wb_scales{pair}")
@@ -151,18 +213,18 @@ def tile_moe_elr_silu_kernel(
             wb_quantised[pair] = (wb_codes, wb_plane)
 
         def hidden(e):
-            gathered, first = slot_planes[e][0], slot_planes[e][2]
             h_rows = []
             for block in range(2):
-                h_rows.append(ring.tile([P, H], BF16, name=f"h_rows{e}_{block}", tag=f"h_rows{block}"))
+                h_rows.append(own([P, H], BF16, f"h_rows{e}_{block}"))
                 h_sum = psum.tile([P, H], F32, name=f"h{e}_{block}", tag=f"h{block}{e % 2}")
+                cols = slice(e % 3 * C + block * P, e % 3 * C + (block + 1) * P)
                 for s in range(PASSES):
                     nc.tensor.matmul_mx(
                         out=h_sum[:],
                         lhsT=slot_words[e][:, s, block * P : (block + 1) * P].bitcast(FP8X4),
-                        lhsT_scale=gathered[4 * s :, first + block * P : first + (block + 1) * P],
-                        rhs=wa_t[e][:, s, :].bitcast(FP8X4),
-                        rhs_scale=wa_planes[e // HALF][:, (e % HALF) * PASSES + s, :],
+                        lhsT_scale=planes[e // 3][4 * s :, cols],
+                        rhs=wa_t[e, s].bitcast(FP8X4),
+                        rhs_scale=wa_plane(e, s),
                         start=(s == 0),
                         stop=(s == PASSES - 1),
                     )
@@ -174,94 +236,79 @@ def tile_moe_elr_silu_kernel(
             return h_rows
 
         def turn(e, h_rows):
-            for a, b in spans(e):
-                blocks = range(a // P, b // P)
-                turned = psum.tile([P, len(blocks), 2, P], F32, name=f"t{e}_{a}", tag=f"t{(e + a // P) % 2}")
-                for place, block in enumerate(blocks):
-                    for v in range(2):
-                        half_row = h_rows[block][:].bitcast(F32)[:, v * P : (v + 1) * P]
-                        nc.tensor.transpose(turned[:, place, v, :], half_row, ident[:])
-                h_grouped[e, a] = own([P, 4 * (b - a)], BF16, f"hb{e}_{a}", tag=f"link{e}_{a}")
-                nc.scalar.copy(
-                    out=h_grouped[e, a][:].bitcast(F32).rearrange("p (g j v) -> p g j v", v=2, j=P),
-                    in_=turned[:].rearrange("p g v j -> p g j v"),
-                )
+            turned = psum.tile([P, 2, 2, P], F32, name=f"t{e}", tag=f"t{e % 2}")
+            for block in range(2):
+                for v in range(2):
+                    half_row = h_rows[block][:].bitcast(F32)[:, v * P : (v + 1) * P]
+                    nc.tensor.transpose(turned[:, block, v, :], half_row, ident[:])
+            h_grouped[e] = own([P, 4 * C], BF16, f"hb{e}")
+            nc.scalar.copy(
+                out=h_grouped[e][:].bitcast(F32).rearrange("p (g j v) -> p g j v", v=2, j=P),
+                in_=turned[:].rearrange("p g v j -> p g j v"),
+            )
 
         def results(e):
-            gathered, moved, first = slot_planes[e]
             wb_codes, wb_plane = wb_quantised[e // 2]
             wb_cols = slice((e % 2) * N, (e % 2 + 1) * N)
-            for a, b in spans(e):
-                h_codes = ring.tile([P, b - a], U32, name=f"hq{e}_{a}", tag="hq", align_bytes=64)
-                h_plane = ring.tile([P, b - a], U8, name=f"hs{e}_{a}", tag="hs", align_bytes=64)
-                nc.vector.quantize_mx(out=h_codes[:].bitcast(FP8X4), scales=h_plane[:], in_=h_grouped[e, a][:])
-                bank = f"t{(e + a // P) % 2}" if e == E - 1 else f"h0{e % 2}"
-                y_sum = psum.tile([P, b - a], F32, name=f"y{e}_{a}", tag=bank)
-                for c in range(a, b, P):
-                    for s in range(PASSES):
-                        plane_cols = slice(first + c, first + c + P)
-                        nc.tensor.matmul_mx(
-                            out=y_sum[:, c - a : c - a + P],
-                            lhsT=w_t[e // 2][:, (e % 2) * PASSES + s, :].bitcast(FP4X4),
-                            lhsT_scale=w_planes[:, e * PASSES + s, :],
-                            rhs=slot_words[e][:, s, c : c + P].bitcast(FP8X4),
-                            rhs_scale=gathered[:, plane_cols] if s == 0 else moved[:, s - 1, plane_cols],
-                            start=(s == 0),
-                            stop=False,
-                        )
+            h_codes = own([P, C], U32, f"hq{e}")
+            h_plane = own([P, C], U8, f"hs{e}")
+            nc.vector.quantize_mx(out=h_codes[:].bitcast(FP8X4), scales=h_plane[:], in_=h_grouped[e][:])
+            y_sum = psum.tile([P, C], F32, name=f"y{e}", tag=f"h{e % 2}1")
+            for c in range(0, C, P):
+                cols = slice(e % 3 * C + c, e % 3 * C + c + P)
+                nc.tensor.matmul_mx(
+                    out=y_sum[:, c : c + P],
+                    lhsT=wb_codes[:, wb_cols].bitcast(FP8X4),
+                    lhsT_scale=wb_plane[:, wb_cols],
+                    rhs=h_codes[:, c : c + P].bitcast(FP8X4),
+                    rhs_scale=h_plane[:, c : c + P],
+                    start=True,
+                    stop=False,
+                )
+                for s in range(PASSES):
                     nc.tensor.matmul_mx(
-                        out=y_sum[:, c - a : c - a + P],
-                        lhsT=wb_codes[:, wb_cols].bitcast(FP8X4),
-                        lhsT_scale=wb_plane[:, wb_cols],
-                        rhs=h_codes[:, c - a : c - a + P].bitcast(FP8X4),
-                        rhs_scale=h_plane[:, c - a : c - a + P],
+                        out=y_sum[:, c : c + P],
+                        lhsT=w_t[e][:, s, :].bitcast(FP4X4),
+                        lhsT_scale=late["ws"][:, e * PASSES + s, :],
+                        rhs=slot_words[e][:, s, c : c + P].bitcast(FP8X4),
+                        rhs_scale=planes[e // 3][:, cols] if s == 0 else shifted[e // 3][:, s - 1, cols],
                         start=False,
-                        stop=True,
+                        stop=(s == PASSES - 1),
                     )
-                nc.scalar.copy(out=y_all[:, e * C + a : e * C + b], in_=y_sum[:])
+            nc.scalar.copy(out=y_all[:, e * C : (e + 1) * C], in_=y_sum[:])
 
-        gather_words(0, own([P, PASSES, C], U32, "xg0"))
-        gather_bytes(0)
-        gather_bytes(1)
-        early_words = own([P, LAG - 1, PASSES, C], U32, "xg_early", tag="after_first_bytes")
         rows = {}
         for e in range(E):
-            if 1 <= e < LAG:
-                gather_words(e, early_words[:, e - 1, :, :])
-            if e == BYTE_GROUPS[2][0]:
-                gather_bytes(2)
-            if e >= LAG:
-                load_wa(e)
-                gather_words(e, own([P, PASSES, C], U32, f"xg{e}", tag=f"link{e - LAG}_0"))
+            gather(e)
             rows[e] = hidden(e)
+            loads_after_hidden(e)
             if e >= 1:
                 turn(e - 1, rows[e - 1])
+                loads_after_turn(e - 1)
+        turn(E - 1, rows[E - 1])
+        for e in range(E):
             if e % 2 == 0:
                 quantise_wb(e // 2)
-            if e == 2:
-                load_pair(2)
-            if e >= LAG - 1:
-                results(e - (LAG - 1))
-        gate_t = held.tile([P, TOP, T], F32, name="gate_t", tag="wa", bufs=WA_BUFS, align_bytes=64)
-        nc.sync.dma_start(out=gate_t[:], in_=gate.rearrange("r p t -> p r t"))
-        turn(E - 1, rows[E - 1])
-        for e in range(E - LAG + 1, E):
             results(e)
 
-        width = T // 2
-        for part in range(2):
-            tokens = slice(part * width, (part + 1) * width)
-            weighted = []
-            for choice in range(TOP):
-                weighted.append(own([P, width], F32, f"prod{part}_{choice}"))
-                nc.vector.tensor_tensor(
-                    weighted[choice][:],
-                    y_all[:].indirect(pos_t[choice][:, part * width // 16 : (part + 1) * width // 16]),
-                    gate_t[:, choice, tokens],
-                    MULT,
-                )
-            two = own([P, width], F32, f"pair{part}")
-            nc.vector.tensor_tensor(two[:], weighted[0][:], weighted[1][:], ADD)
-            total = own([P, width], F32, f"total{part}")
-            nc.vector.tensor_tensor(total[:], two[:], weighted[2][:], ADD)
+        weighted = [own([P, T], F32, f"prod{choice}") for choice in range(TOP)]
+        halves = [slice(0, T // 2), slice(T // 2, T)]
+
+        def fetch(choice, tokens):
+            nc.vector.tensor_tensor(
+                weighted[choice][:, tokens],
+                y_all[:].indirect(pos_t[choice][:, tokens.start // 16 : tokens.stop // 16]),
+                gate_t[choice][:, tokens],
+                MULT,
+            )
+
+        fetch(0, slice(0, T))
+        fetch(1, slice(0, T))
+        fetch(2, halves[0])
+        two = own([P, T], F32, "two")
+        nc.vector.tensor_tensor(two[:], weighted[0][:], weighted[1][:], ADD)
+        fetch(2, halves[1])
+        for part, tokens in enumerate(halves):
+            total = own([P, T // 2], F32, f"total{part}")
+            nc.vector.tensor_tensor(total[:], two[:, tokens], weighted[2][:, tokens], ADD)
             nc.sync.dma_start(out=out[:, tokens], in_=total[:])

@@ -22,7 +22,9 @@ MULT = mybir.AluOpType.mult
 ADD = mybir.AluOpType.add
 
 PLANE_ROWS = 100
-DENSE = 8
+HALF = SLOTS // 2
+BYTE_WINDOW = 512
+LATE = 17408
 
 
 def tile_moe_elr_silu_kernel(
@@ -31,215 +33,165 @@ def tile_moe_elr_silu_kernel(
     nc = tc.nc
     with ExitStack() as ctx:
         held = ctx.enter_context(tc.tile_pool(name="held", bufs=1))
+        placed = ctx.enter_context(tc.tile_pool(name="placed", bufs=1))
         psum = ctx.enter_context(tc.psum_pool(name="psum", bufs=1))
 
         def own(shape, dtype, name, tag=None):
             return held.tile(shape, dtype, name=name, tag=tag or name, align_bytes=64)
 
-        xs_first = own([P, T], U8, "xs_first")
-        nc.gpsimd.memset(xs_first[:].bitcast(I32), 0)
-        offs_t = held.tile([P, SLOTS // 16], U16, name="offs_t")
-        nc.sync.dma_start(offs_t[:], offs)
+        def at(offset, shape, dtype, name):
+            return placed.tile(shape, dtype, name=name, tag=name, align_bytes=64, offset=offset)
+
+        def zeroed(shape, name):
+            plane = own(shape, U8, name)
+            nc.vector.memset(plane[:].bitcast(I32), 0)
+            return plane
 
         was_src = wa_scales.bitcast(I32).rearrange("e s (q r) c -> q (e s) r c", r=4)
         wa_src = wa_words.rearrange("e s p i d -> e p s (i d)").bitcast(I32)
         xw_src = x_words.rearrange("s p t d -> p s (t d)").bitcast(I32)
         xs_src = x_scales.bitcast(I32).rearrange("s (q r) c -> q s r c", r=4)
-        wa_t = {}
-
-        def load_dense(plane, group, q):
-            rows = was_src[q, DENSE * group : min(DENSE * (group + 1), E * PASSES)]
-            nc.sync.dma_start(out=plane[32 * q : 32 * q + 4 * rows.shape[0], :].bitcast(I32), in_=rows)
-
-        def load_wa(e, words):
-            nc.sync.dma_start(out=words.rearrange("p (s c) -> p s c", s=PASSES), in_=wa_src[e])
-            for s in range(PASSES):
-                wa_t[e, s] = words[:, s * H : (s + 1) * H]
-
-        def move_up(queue, group, rows):
-            queue.dma_start(
-                out=raised[group, rows][0 : P - rows, :].bitcast(I32), in_=dense[group][rows:P, :].bitcast(I32)
-            )
-
-        def load_xs(queue, q):
-            queue.dma_start(out=xs_first[32 * q : 32 * q + 4 * PASSES, :].bitcast(I32), in_=xs_src[q])
-
         w_src = w_words.bitcast(I32).rearrange("e s p c -> p (e s) c")
         wb_src = wb.rearrange("(g e) (p j) n -> g p e (j n)", e=2, j=4)
         ws_src = w_scales.bitcast(I32).rearrange("e s (q r) c -> r q (e s) c", r=4)
-        w_t, wb_raw, gate_t, late, pos_t = {}, {}, [], {}, []
 
-        def load_wb(pair, tag):
-            wb_raw[pair] = own([P, 2, 4 * N], F32, f"wb_raw{pair}", tag=tag)[:]
-            nc.sync.dma_start(out=wb_raw[pair], in_=wb_src[pair])
+        xs = at(0, [P, BYTE_WINDOW], U8, "xs")
+        nc.gpsimd.memset(xs[:, 0:T].bitcast(I32), 0)
+        offs_t = held.tile([P, SLOTS // 16], U16, name="offs_t")
+        nc.sync.dma_start(offs_t[:], offs)
 
-        def load_w(e0, e1, tag):
-            words = own([P, (e1 - e0) * PASSES, 2 * N], U8, f"w{e0}", tag=tag)
-            nc.sync.dma_start(out=words[:].bitcast(I32), in_=w_src[:, e0 * PASSES : e1 * PASSES, :])
-            for e in range(e0, e1):
-                w_t[e] = words[:, (e - e0) * PASSES : (e - e0 + 1) * PASSES, :]
+        def load_xs(queue, q, s0, s1):
+            queue.dma_start(out=xs[32 * q + 4 * s0 : 32 * q + 4 * s1, 0:T].bitcast(I32), in_=xs_src[q, s0:s1])
 
-        for q in range(4):
-            load_xs(nc.gpsimd if q < 2 else nc.scalar, q)
-        dense = [own([P, H], U8, "dense0")[:]]
-        load_dense(dense[0], 0, 0)
-        x_rest = own([P, PASSES, T], I32, "x_rest")
-        nc.sync.dma_start(out=x_rest[:, 0:2, :], in_=xw_src[:, 0:2, :])
-        load_dense(dense[0], 0, 1)
-        x_last = own([P, T], I32, "x_last")
-        nc.sync.dma_start(out=x_last[:], in_=xw_src[:, 2, :])
-        load_wa(0, own([P, PASSES * H], I32, "wa0")[:])
-        load_dense(dense[0], 0, 2)
-        load_dense(dense[0], 0, 3)
-        load_wa(1, own([P, PASSES * H], I32, "wa1")[:])
+        load_xs(nc.gpsimd, 0, 0, 3)
 
+        def load_planes(plane, numbers, quadrants=range(4), queue=nc.sync):
+            for q in quadrants:
+                rows = was_src[q, numbers]
+                queue.dma_start(out=plane[32 * q : 32 * q + 4 * rows.shape[0], :].bitcast(I32), in_=rows)
+
+        wa_t, wb_raw, pos_t = {}, {}, []
+
+        def load_wa(e):
+            wa_t[e] = at(LATE, [P, PASSES, H], I32, "wa4") if e == 4 else own([P, PASSES, H], I32, f"wa{e}")
+            nc.sync.dma_start(out=wa_t[e][:], in_=wa_src[e])
+
+        def load_wb(pair):
+            wb_raw[pair] = own([P, 2, 4 * N], F32, f"wb_raw{pair}")
+            nc.sync.dma_start(out=wb_raw[pair][:], in_=wb_src[pair])
+
+        dense = [own([P, H], U8, f"dense{g}") for g in range(2)]
+        load_planes(dense[0], slice(0, 8), range(4), nc.scalar)
+        load_xs(nc.sync, 1, 0, 2)
+        load_xs(nc.sync, 2, 0, 2)
+        x_t = own([P, PASSES, T], I32, "x_t")
+        nc.sync.dma_start(out=x_t[:], in_=xw_src)
+        load_xs(nc.sync, 3, 0, 2)
+        for q in range(1, 4):
+            load_xs(nc.sync, q, 2, 3)
+        wa_first = own([P, H], I32, "wa_first")
+        nc.sync.dma_start(out=wa_first[:], in_=wa_src[0, :, 0, :])
+        wa_t[0] = own([P, PASSES - 1, H], I32, "wa0")
+        nc.sync.dma_start(out=wa_t[0][:], in_=wa_src[0, :, 1:, :])
+        raised = [zeroed([P, H], f"raised{g}") for g in range(2)]
+        odd = zeroed([P, H], "odd")
+        ws = zeroed([P, E * PASSES, N], "ws")
+        shifted = zeroed([P, PASSES - 1, SLOTS], "shifted")
+        warm = own([P, 1], F32, "warm")
+        nc.scalar.activation(out=warm[:], in_=raised[1][:, 0:4].bitcast(F32), func=SILU)
         ident = own([P, P], F32, "ident")
         make_identity(nc, ident[:])
-        raised = {}
-        for key in ((0, 16), (1, 8), (1, 24)):
-            raised[key] = own([P, H], U8, f"raised{key[0]}_{key[1]}")
-            nc.vector.memset(raised[key][:].bitcast(I32), 0)
-        warm = own([P, 1], F32, "warm")
-        nc.scalar.activation(out=warm[:], in_=raised[1, 8][:, 0:4].bitcast(F32), func=SILU)
-        move_up(nc.scalar, 0, 16)
-        load_wa(2, own([P, PASSES * H], I32, "wa2")[:])
-        for choice, pos in enumerate((pos1, pos2, pos3)):
-            pos_t.append(held.tile([P, T // 16], U16, name=f"pos_t{choice}"))
-            nc.sync.dma_start(pos_t[choice][:], pos)
-        load_w(0, 4, None)
+
+        def raise_planes(g):
+            nc.sync.dma_start(out=raised[g][0 : P - 16, :].bitcast(I32), in_=dense[g][16:P, :].bitcast(I32))
+
+        load_wa(1)
+        raise_planes(0)
+        load_wa(2)
+        load_planes(odd, slice(8, 18, 9))
+        load_wb(0)
+        load_wa(3)
+        load_planes(dense[1], slice(9, 17))
+        load_wa(4)
+        load_wa(5)
+        raise_planes(1)
+        load_wb(1)
+        load_wb(2)
+        w_t = own([P, E * PASSES, 2 * N], U8, "w_t")
 
         def wa_plane(e, s):
-            group, place = divmod(e * PASSES + s, DENSE)
-            moved = [rows for g, rows in raised if g == group and rows <= 4 * place]
-            if not moved:
-                return dense[group][4 * place :, :]
-            return raised[group, max(moved)][4 * place - max(moved) :, :]
-
-        shifted = {}
-
-        def shift(part, tag):
-            shifted[part] = own([P, PASSES - 1, SLOTS // 2], U8, f"shifted{part}", tag=tag)
-            nc.gpsimd.memset(shifted[part][:].bitcast(I32), 0)
-            for s in range(1, PASSES):
-                nc.sync.dma_start(
-                    out=shifted[part][0:PLANE_ROWS, s - 1, :].bitcast(I32),
-                    in_=planes[part][4 * s : 4 * s + PLANE_ROWS, :].bitcast(I32),
-                )
-
-        def loads_after_hidden(e):
-            if e == 0:
-                both = own([P, PASSES * H + H // 4], I32, "wa3", tag="wa0")
-                load_wa(3, both[:, : PASSES * H])
-                dense.append(both[:, PASSES * H :].bitcast(U8))
-                for q in range(4):
-                    load_dense(dense[1], 1, q)
-            if e == 1:
-                load_wb(0, "dense0")
-                load_wa(4, own([P, PASSES * H], I32, "wa4", tag="wa1")[:])
-                move_up(nc.sync, 1, 8)
-                move_up(nc.sync, 1, 24)
-            if e == 2:
-                load_wa(5, own([P, PASSES * H], I32, "wa5", tag="wa2")[:])
-
-        def loads_after_turn(e):
-            if e == 0:
-                dense.append(own([P, H], U8, "dense2", tag="h_rows0_0")[:])
-                nc.gpsimd.memset(dense[2].bitcast(I32), 0)
-                for q in range(4):
-                    load_dense(dense[2], 2, q)
-            if e == 1:
-                load_wb(1, "h_rows1_0")
-            if e == 2:
-                late["ws"] = own([P, E * PASSES, N], U8, "ws", tag="h_rows2_0")
-                nc.gpsimd.memset(late["ws"][:].bitcast(I32), 0)
-                load_wb(2, "wa0")
-                for r in range(4):
-                    nc.sync.dma_start(out=late["ws"][r:P:32, :, :].bitcast(I32), in_=ws_src[r])
-                shift(0, "h_rows2_1")
-            if e == 3:
-                load_w(4, 6, "h_rows3_0")
-            if e == 4:
-                shift(1, "wa1")
-                gates = own([P, TOP, T], F32, "gates", tag="h_rows4_0")
-                for choice in range(TOP):
-                    nc.sync.dma_start(out=gates[:, choice, :], in_=gate[choice])
-                    gate_t.append(gates[:, choice, :])
+            group, place = divmod(e * PASSES + s, 9)
+            if place == 8:
+                return odd[4 * group :, :]
+            return (dense if place < 4 else raised)[group][4 * (place % 4) :, :]
 
         y_all = own([P, SLOTS], F32, "y_all")
-        planes = [own([P, SLOTS // 2], U8, f"planes{part}") for part in range(2)]
-        slot_words, h_grouped, wb_quantised = {}, {}, {}
+        groups = [(e, e + 1) for e in range(E)]
+        planes_t = own([P, SLOTS], U8, "planes")
+        xs_later = own([P, BYTE_WINDOW], U8, "xs_later")
+        words_first = own([P, C], U32, "words_first")
+        words_later = at(0, [P, E * PASSES - 1, C], U32, "words_later")
+        planes, words, moved = {}, {}, {}
+        for e in range(E):
+            planes[e] = planes_t[:, e * C : (e + 1) * C]
+            moved[e] = shifted[:, :, e * C : (e + 1) * C]
+            for s in range(PASSES):
+                words[e, s] = words_later[:, e * PASSES + s - 1, :] if e + s else words_first[:]
+        h_rows, h_grouped, wb_grouped, wb_quantised = {}, {}, {}, {}
 
         def offsets(first, last):
             return offs_t[:, first // 16 : last // 16]
 
-        def gather(e):
-            cols = slice(e % 3 * C, (e % 3 + 1) * C)
-            if e == 0:
-                slot_words[0] = own([P, PASSES, C], U32, "xg0")[:]
-                windows = (x_rest[:, 0, :], x_rest[:, 1, :], x_last[:])
-                nc.vector.tensor_copy(x_rest[:, 2, :], x_last[:])
-            else:
-                slot_words[e] = late["words"][:, e - 1, :, :]
-                windows = [x_rest[:, s, :] for s in range(PASSES)]
-            byte_window = xs_first if e == 0 else late["xs"]
-            nc.vector.tensor_copy(planes[e // 3][:, cols], byte_window[:].indirect(offsets(e * C, (e + 1) * C)))
-            for s in range(PASSES):
-                nc.vector.tensor_copy(
-                    slot_words[e][:, s, :], windows[s].bitcast(U32).indirect(offsets(e * C, (e + 1) * C))
-                )
-            if e == 0:
-                late["xs"] = own([P, T], U8, "xs_rest", tag="x_last")
-                nc.vector.tensor_copy(late["xs"][:].bitcast(I32), xs_first[:].bitcast(I32))
-                late["words"] = own([P, E - 1, PASSES, C], U32, "xg_late", tag="xs_first")
+        def gather_bytes(g):
+            e0, e1 = groups[g]
+            window = xs_later if g else xs
+            nc.vector.tensor_copy(planes_t[:, e0 * C : e1 * C], window[:].indirect(offsets(e0 * C, e1 * C)))
 
-        def quantise_wb(pair):
-            wb_grouped = own([P, 2, N * 4], BF16, f"wb_bf{pair}", tag=("h_rows1_1", "h_rows3_1", None)[pair])
-            if pair < 2:
-                for member in range(2):
-                    nc.scalar.copy(
-                        out=wb_grouped[:, member, :].rearrange("p (c m j) -> p c j m", m=4, j=4),
-                        in_=wb_raw[pair][:, member, :].rearrange("p (j c m) -> p c j m", m=4, j=4),
-                    )
-            else:
-                nc.vector.tensor_copy(
-                    out=wb_grouped[:].rearrange("p e (c m j) -> p e c j m", m=4, j=4),
-                    in_=wb_raw[pair].rearrange("p e (j c m) -> p e c j m", m=4, j=4),
+        def shift(cols):
+            for s in range(1, PASSES):
+                nc.sync.dma_start(
+                    out=shifted[0:PLANE_ROWS, s - 1, cols].bitcast(I32),
+                    in_=planes_t[4 * s : 4 * s + PLANE_ROWS, cols].bitcast(I32),
                 )
-            wb_codes = own([P, 2 * N], U32, f"wb_codes{pair}")
-            wb_plane = own([P, 2 * N], U8, f"wb_scales{pair}")
-            nc.vector.quantize_mx(
-                out=wb_codes[:].bitcast(FP8X4), scales=wb_plane[:], in_=wb_grouped[:].rearrange("p e c -> p (e c)")
-            )
-            wb_quantised[pair] = (wb_codes, wb_plane)
+
+        def gather_words(e, s):
+            nc.vector.tensor_copy(words[e, s], x_t[:, s, :].bitcast(U32).indirect(offsets(e * C, (e + 1) * C)))
+
+        def wa_pass(e, s):
+            if e > 0:
+                return wa_t[e][:, s, :]
+            return wa_first[:] if s == 0 else wa_t[0][:, s - 1, :]
 
         def hidden(e):
-            h_rows = []
-            for block in range(2):
-                h_rows.append(own([P, H], BF16, f"h_rows{e}_{block}"))
-                h_sum = psum.tile([P, H], F32, name=f"h{e}_{block}", tag=f"h{block}{e % 2}")
-                cols = slice(e % 3 * C + block * P, e % 3 * C + (block + 1) * P)
-                for s in range(PASSES):
-                    nc.tensor.matmul_mx(
-                        out=h_sum[:],
-                        lhsT=slot_words[e][:, s, block * P : (block + 1) * P].bitcast(FP8X4),
-                        lhsT_scale=planes[e // 3][4 * s :, cols],
-                        rhs=wa_t[e, s].bitcast(FP8X4),
-                        rhs_scale=wa_plane(e, s),
-                        start=(s == 0),
-                        stop=(s == PASSES - 1),
-                    )
-                nc.scalar.activation(
-                    out=h_rows[block][:].rearrange("p (v m d) -> p v m d", v=2, d=2),
-                    in_=h_sum[:].rearrange("p (m v d) -> p v m d", v=2, d=2),
-                    func=SILU,
+            sums = [psum.tile([P, H], F32, name=f"h{e}_{b}", tag=f"bank{(2 * e + b) % 8}") for b in range(2)]
+            order = [(b, s) for b in range(2) for s in range(PASSES)]
+            if e == 0:
+                order = sorted(order, key=lambda step: step[1])
+            for block, s in order:
+                if e >= 2 and (block, s) == (1, 0):
+                    turn(e - 2)
+                nc.tensor.matmul_mx(
+                    out=sums[block][:],
+                    lhsT=words[e, s][:, block * P : (block + 1) * P].bitcast(FP8X4),
+                    lhsT_scale=planes[e][4 * s :, block * P : (block + 1) * P],
+                    rhs=wa_pass(e, s).bitcast(FP8X4),
+                    rhs_scale=wa_plane(e, s),
+                    start=(s == 0),
+                    stop=(s == PASSES - 1),
                 )
-            return h_rows
+                if s == PASSES - 1:
+                    h_rows[e, block] = own([P, H], BF16, f"h_rows{e}_{block}")
+                    nc.scalar.activation(
+                        out=h_rows[e, block][:].rearrange("p (v m d) -> p v m d", v=2, d=2),
+                        in_=sums[block][:].rearrange("p (m v d) -> p v m d", v=2, d=2),
+                        func=SILU,
+                    )
 
-        def turn(e, h_rows):
-            turned = psum.tile([P, 2, 2, P], F32, name=f"t{e}", tag=f"t{e % 2}")
+        def turn(e):
+            turned = psum.tile([P, 2, 2, P], F32, name=f"t{e}", tag=f"bank{(2 * e + 2) % 8}")
             for block in range(2):
                 for v in range(2):
-                    half_row = h_rows[block][:].bitcast(F32)[:, v * P : (v + 1) * P]
+                    half_row = h_rows[e, block][:].bitcast(F32)[:, v * P : (v + 1) * P]
                     nc.tensor.transpose(turned[:, block, v, :], half_row, ident[:])
             h_grouped[e] = own([P, 4 * C], BF16, f"hb{e}")
             nc.scalar.copy(
@@ -247,48 +199,96 @@ def tile_moe_elr_silu_kernel(
                 in_=turned[:].rearrange("p g v j -> p g j v"),
             )
 
-        def results(e):
-            wb_codes, wb_plane = wb_quantised[e // 2]
-            wb_cols = slice((e % 2) * N, (e % 2 + 1) * N)
-            h_codes = own([P, C], U32, f"hq{e}")
-            h_plane = own([P, C], U8, f"hs{e}")
-            nc.vector.quantize_mx(out=h_codes[:].bitcast(FP8X4), scales=h_plane[:], in_=h_grouped[e][:])
-            y_sum = psum.tile([P, C], F32, name=f"y{e}", tag=f"h{e % 2}1")
-            for c in range(0, C, P):
-                cols = slice(e % 3 * C + c, e % 3 * C + c + P)
-                nc.tensor.matmul_mx(
-                    out=y_sum[:, c : c + P],
-                    lhsT=wb_codes[:, wb_cols].bitcast(FP8X4),
-                    lhsT_scale=wb_plane[:, wb_cols],
-                    rhs=h_codes[:, c : c + P].bitcast(FP8X4),
-                    rhs_scale=h_plane[:, c : c + P],
-                    start=True,
-                    stop=False,
+        def cast_wb(e):
+            if e < 2:
+                wb_grouped[e] = own([P, N * 4], BF16, f"wb_bf{e}", tag=f"h_rows{e + 1}_0")
+                nc.scalar.copy(
+                    out=wb_grouped[e][:].rearrange("p (c m j) -> p c j m", m=4, j=4),
+                    in_=wb_raw[0][:, e, :].rearrange("p (j c m) -> p c j m", m=4, j=4),
                 )
+            else:
+                wb_grouped[e] = own([P, 2 * N * 4], BF16, f"wb_bf{e}")
+                nc.gpsimd.tensor_copy(
+                    out=wb_grouped[e][:].rearrange("p (e n j) -> p e n j", e=2, j=4),
+                    in_=wb_raw[e // 2][:].rearrange("p e (j n) -> p e n j", j=4),
+                )
+
+        def quantise(values, width, name, offset=None):
+            codes = at(offset, [P, width], U32, f"{name}_codes") if offset else own([P, width], U32, f"{name}_codes")
+            plane = own([P, width], U8, f"{name}_plane")
+            nc.vector.quantize_mx(out=codes[:].bitcast(FP8X4), scales=plane[:], in_=values[:])
+            return codes, plane
+
+        def results(e):
+            if e in wb_grouped:
+                width = N if e < 2 else 2 * N
+                codes, plane = quantise(wb_grouped[e], width, f"wb{e}")
+                for n0 in range(0, width, N):
+                    wb_quantised[e + n0 // N] = (codes[:, n0 : n0 + N], plane[:, n0 : n0 + N])
+            wb_codes, wb_plane = wb_quantised[e]
+            h_codes, h_plane = quantise(h_grouped[e], C, f"h{e}")
+            y_sum = psum.tile([P, C], F32, name=f"y{e}", tag=f"bank{(5, 6, 7, 0, 1, 3)[e]}")
+            last = True
+
+            def adapter():
+                nc.tensor.matmul_mx(
+                    out=y_sum[:],
+                    lhsT=wb_codes.bitcast(FP8X4),
+                    lhsT_scale=wb_plane,
+                    rhs=h_codes[:].bitcast(FP8X4),
+                    rhs_scale=h_plane[:],
+                    start=not last,
+                    stop=last,
+                )
+
+            if not last:
+                adapter()
+            for c in range(0, C, P):
                 for s in range(PASSES):
                     nc.tensor.matmul_mx(
                         out=y_sum[:, c : c + P],
-                        lhsT=w_t[e][:, s, :].bitcast(FP4X4),
-                        lhsT_scale=late["ws"][:, e * PASSES + s, :],
-                        rhs=slot_words[e][:, s, c : c + P].bitcast(FP8X4),
-                        rhs_scale=planes[e // 3][:, cols] if s == 0 else shifted[e // 3][:, s - 1, cols],
-                        start=False,
-                        stop=(s == PASSES - 1),
+                        lhsT=w_t[:, e * PASSES + s, :].bitcast(FP4X4),
+                        lhsT_scale=ws[:, e * PASSES + s, :],
+                        rhs=words[e, s][:, c : c + P].bitcast(FP8X4),
+                        rhs_scale=planes[e][:, c : c + P] if s == 0 else moved[e][:, s - 1, c : c + P],
+                        start=last and c == 0 and s == 0,
+                        stop=not last and c == P and s == PASSES - 1,
                     )
+            if last:
+                adapter()
             nc.scalar.copy(out=y_all[:, e * C : (e + 1) * C], in_=y_sum[:])
 
-        rows = {}
+        gates = own([P, TOP, T], F32, "gates")
         for e in range(E):
-            gather(e)
-            rows[e] = hidden(e)
-            loads_after_hidden(e)
-            if e >= 1:
-                turn(e - 1, rows[e - 1])
-                loads_after_turn(e - 1)
-        turn(E - 1, rows[E - 1])
-        for e in range(E):
-            if e % 2 == 0:
-                quantise_wb(e // 2)
+            if e == 0:
+                gather_words(0, 0)
+                gather_bytes(0)
+                nc.vector.tensor_copy(xs_later[:].bitcast(I32), xs[:].bitcast(I32))
+            else:
+                gather_bytes(e)
+            if e == 2:
+                shift(slice(0, HALF))
+                for r in range(4):
+                    nc.sync.dma_start(out=ws[r:P:32, :, :].bitcast(I32), in_=ws_src[r])
+                nc.sync.dma_start(out=w_t[:].bitcast(I32), in_=w_src)
+            if e == 5:
+                shift(slice(HALF, SLOTS))
+                for choice, pos in enumerate((pos1, pos2, pos3)):
+                    pos_t.append(held.tile([P, T // 16], U16, name=f"pos_t{choice}"))
+                    nc.sync.dma_start(pos_t[choice][:], pos)
+                nc.sync.dma_start(out=gates[:], in_=gate.rearrange("r p t -> p r t"))
+            for s in range(1 if e == 0 else 0, PASSES):
+                gather_words(e, s)
+            hidden(e)
+            if e in (3, 4):
+                cast_wb(e - 3)
+        turn(E - 2)
+        cast_wb(2)
+        cast_wb(4)
+        results(0)
+        results(1)
+        turn(E - 1)
+        for e in range(2, E):
             results(e)
 
         weighted = [own([P, T], F32, f"prod{choice}") for choice in range(TOP)]
@@ -298,7 +298,7 @@ def tile_moe_elr_silu_kernel(
             nc.vector.tensor_tensor(
                 weighted[choice][:, tokens],
                 y_all[:].indirect(pos_t[choice][:, tokens.start // 16 : tokens.stop // 16]),
-                gate_t[choice][:, tokens],
+                gates[:, choice, tokens],
                 MULT,
             )
 

@@ -109,12 +109,12 @@ def tile_moe_elr_silu_kernel(
         raise_planes(0)
         load_wa(2)
         load_planes(odd, slice(8, 18, 9))
-        load_wb(0)
         load_wa(3)
         load_planes(dense[1], slice(9, 17))
         load_wa(4)
         load_wa(5)
         raise_planes(1)
+        load_wb(0)
         load_wb(1)
         load_wb(2)
         w_t = own([P, E * PASSES, 2 * N], U8, "w_t")
@@ -200,18 +200,11 @@ def tile_moe_elr_silu_kernel(
             )
 
         def cast_wb(e):
-            if e < 2:
-                wb_grouped[e] = own([P, N * 4], BF16, f"wb_bf{e}", tag=f"h_rows{e + 1}_0")
-                nc.scalar.copy(
-                    out=wb_grouped[e][:].rearrange("p (c m j) -> p c j m", m=4, j=4),
-                    in_=wb_raw[0][:, e, :].rearrange("p (j c m) -> p c j m", m=4, j=4),
-                )
-            else:
-                wb_grouped[e] = own([P, 2 * N * 4], BF16, f"wb_bf{e}")
-                nc.gpsimd.tensor_copy(
-                    out=wb_grouped[e][:].rearrange("p (e n j) -> p e n j", e=2, j=4),
-                    in_=wb_raw[e // 2][:].rearrange("p e (j n) -> p e n j", j=4),
-                )
+            wb_grouped[e] = own([P, 2 * N * 4], BF16, f"wb_bf{e}")
+            nc.vector.tensor_copy(
+                out=wb_grouped[e][:].rearrange("p (e c m j) -> p e c j m", e=2, m=4, j=4),
+                in_=wb_raw[e // 2][:].rearrange("p e (j c m) -> p e c j m", m=4, j=4),
+            )
 
         def quantise(values, width, name, offset=None):
             codes = at(offset, [P, width], U32, f"{name}_codes") if offset else own([P, width], U32, f"{name}_codes")
@@ -221,7 +214,7 @@ def tile_moe_elr_silu_kernel(
 
         def results(e):
             if e in wb_grouped:
-                width = N if e < 2 else 2 * N
+                width = 2 * N
                 codes, plane = quantise(wb_grouped[e], width, f"wb{e}")
                 for n0 in range(0, width, N):
                     wb_quantised[e + n0 // N] = (codes[:, n0 : n0 + N], plane[:, n0 : n0 + N])
@@ -280,9 +273,8 @@ def tile_moe_elr_silu_kernel(
             for s in range(1 if e == 0 else 0, PASSES):
                 gather_words(e, s)
             hidden(e)
-            if e in (3, 4):
-                cast_wb(e - 3)
         turn(E - 2)
+        cast_wb(0)
         cast_wb(2)
         cast_wb(4)
         results(0)

@@ -18,6 +18,7 @@ U8 = mybir.dt.uint8
 FP8X4 = mybir.dt.float8_e4m3fn_x4
 FP4X4 = mybir.dt.float4_e2m1fn_x4
 SILU = mybir.ActivationFunctionType.Silu
+COPY = mybir.ActivationFunctionType.Copy
 MULT = mybir.AluOpType.mult
 ADD = mybir.AluOpType.add
 
@@ -221,34 +222,25 @@ def tile_moe_elr_silu_kernel(
             wb_codes, wb_plane = wb_quantised[e]
             h_codes, h_plane = quantise(h_grouped[e], C, f"h{e}")
             y_sum = psum.tile([P, C], F32, name=f"y{e}", tag=f"bank{(5, 6, 7, 0, 1, 3)[e]}")
-            last = True
-
-            def adapter():
+            for s in range(PASSES):
                 nc.tensor.matmul_mx(
                     out=y_sum[:],
-                    lhsT=wb_codes.bitcast(FP8X4),
-                    lhsT_scale=wb_plane,
-                    rhs=h_codes[:].bitcast(FP8X4),
-                    rhs_scale=h_plane[:],
-                    start=not last,
-                    stop=last,
+                    lhsT=w_t[:, e * PASSES + s, :].bitcast(FP4X4),
+                    lhsT_scale=ws[:, e * PASSES + s, :],
+                    rhs=words[e, s].bitcast(FP8X4),
+                    rhs_scale=planes[e] if s == 0 else moved[e][:, s - 1, :],
+                    start=(s == 0),
+                    stop=False,
                 )
-
-            if not last:
-                adapter()
-            for c in range(0, C, P):
-                for s in range(PASSES):
-                    nc.tensor.matmul_mx(
-                        out=y_sum[:, c : c + P],
-                        lhsT=w_t[:, e * PASSES + s, :].bitcast(FP4X4),
-                        lhsT_scale=ws[:, e * PASSES + s, :],
-                        rhs=words[e, s][:, c : c + P].bitcast(FP8X4),
-                        rhs_scale=planes[e][:, c : c + P] if s == 0 else moved[e][:, s - 1, c : c + P],
-                        start=last and c == 0 and s == 0,
-                        stop=not last and c == P and s == PASSES - 1,
-                    )
-            if last:
-                adapter()
+            nc.tensor.matmul_mx(
+                out=y_sum[:],
+                lhsT=wb_codes.bitcast(FP8X4),
+                lhsT_scale=wb_plane,
+                rhs=h_codes[:].bitcast(FP8X4),
+                rhs_scale=h_plane[:],
+                start=False,
+                stop=True,
+            )
             nc.scalar.copy(out=y_all[:, e * C : (e + 1) * C], in_=y_sum[:])
 
         gates = own([P, TOP, T], F32, "gates")
@@ -283,23 +275,22 @@ def tile_moe_elr_silu_kernel(
         for e in range(2, E):
             results(e)
 
-        weighted = [own([P, T], F32, f"prod{choice}") for choice in range(TOP)]
         halves = [slice(0, T // 2), slice(T // 2, T)]
-
-        def fetch(choice, tokens):
-            nc.vector.tensor_tensor(
-                weighted[choice][:, tokens],
-                y_all[:].indirect(pos_t[choice][:, tokens.start // 16 : tokens.stop // 16]),
-                gates[:, choice, tokens],
-                MULT,
+        picked = [own([P, T], F32, f"picked{choice}") for choice in range(1, TOP)]
+        weighted = [own([P, T], F32, f"weighted{choice}") for choice in range(TOP)]
+        nc.vector.tensor_tensor(weighted[0][:], y_all[:].indirect(pos_t[0][:]), gates[:, 0, :], MULT)
+        nc.scalar.activation(out=picked[0][:], in_=y_all[:].indirect(pos_t[1][:]), func=COPY)
+        for tokens in halves:
+            nc.scalar.activation(
+                out=picked[1][:, tokens],
+                in_=y_all[:].indirect(pos_t[2][:, tokens.start // 16 : tokens.stop // 16]),
+                func=COPY,
             )
-
-        fetch(0, slice(0, T))
-        fetch(1, slice(0, T))
-        fetch(2, halves[0])
         two = own([P, T], F32, "two")
+        nc.vector.tensor_tensor(weighted[1][:], picked[0][:], gates[:, 1, :], MULT)
+        nc.vector.tensor_tensor(weighted[2][:, halves[0]], picked[1][:, halves[0]], gates[:, 2, halves[0]], MULT)
         nc.vector.tensor_tensor(two[:], weighted[0][:], weighted[1][:], ADD)
-        fetch(2, halves[1])
+        nc.vector.tensor_tensor(weighted[2][:, halves[1]], picked[1][:, halves[1]], gates[:, 2, halves[1]], MULT)
         for part, tokens in enumerate(halves):
             total = own([P, T // 2], F32, f"total{part}")
             nc.vector.tensor_tensor(total[:], two[:, tokens], weighted[2][:, tokens], ADD)

@@ -23,9 +23,18 @@ MULT = mybir.AluOpType.mult
 ADD = mybir.AluOpType.add
 
 PLANE_ROWS = 100
+LAST_WA = (E * PASSES - 1) * C * 4
+RAISED_FIRST = LAST_WA + (E + 1) * C * 4 + 768
+DENSE_SECOND = RAISED_FIRST + 256 + 2 * H
+RAISED_SECOND = DENSE_SECOND + 2 * H + 768
+LAST_WB = RAISED_SECOND + 256 + 2 * H
+TURN_BANKS = (3, 6, 1, 7, 5, 6)
+HELD_ROWS = {(1, 1): RAISED_FIRST - 768, (2, 0): RAISED_FIRST + 256, (3, 1): DENSE_SECOND}
+DEFERRED = ((1, 1), (3, 1))
+W_PARTS = ((0, 3), (3, 6))
 HALF = SLOTS // 2
-BYTE_WINDOW = 512
-LATE = 17408
+Y_GROUPS = ((0, 1), (2, 3), (4,), (5,))
+Y_BANKS = (3, 2, 0, 1)
 
 
 def tile_moe_elr_silu_kernel(
@@ -43,8 +52,8 @@ def tile_moe_elr_silu_kernel(
         def at(offset, shape, dtype, name):
             return placed.tile(shape, dtype, name=name, tag=name, align_bytes=64, offset=offset)
 
-        def zeroed(shape, name):
-            plane = own(shape, U8, name)
+        def zeroed(shape, name, offset=None):
+            plane = at(offset, shape, U8, name) if offset else own(shape, U8, name)
             nc.vector.memset(plane[:].bitcast(I32), 0)
             return plane
 
@@ -56,33 +65,43 @@ def tile_moe_elr_silu_kernel(
         wb_src = wb.rearrange("(g e) (p j) n -> g p e (j n)", e=2, j=4)
         ws_src = w_scales.bitcast(I32).rearrange("e s (q r) c -> r q (e s) c", r=4)
 
-        xs = at(0, [P, BYTE_WINDOW], U8, "xs")
-        nc.gpsimd.memset(xs[:, 0:T].bitcast(I32), 0)
+        xs = at(0, [P, T], U8, "xs")
+        nc.gpsimd.memset(xs[:].bitcast(I32), 0)
         offs_t = held.tile([P, SLOTS // 16], U16, name="offs_t")
         nc.sync.dma_start(offs_t[:], offs)
 
         def load_xs(queue, q, s0, s1):
-            queue.dma_start(out=xs[32 * q + 4 * s0 : 32 * q + 4 * s1, 0:T].bitcast(I32), in_=xs_src[q, s0:s1])
+            queue.dma_start(out=xs[32 * q + 4 * s0 : 32 * q + 4 * s1, :].bitcast(I32), in_=xs_src[q, s0:s1])
 
         load_xs(nc.gpsimd, 0, 0, 3)
 
-        def load_planes(plane, numbers, quadrants=range(4), queue=nc.sync):
-            for q in quadrants:
+        def load_planes(plane, numbers, queue=nc.sync):
+            for q in range(4):
                 rows = was_src[q, numbers]
                 queue.dma_start(out=plane[32 * q : 32 * q + 4 * rows.shape[0], :].bitcast(I32), in_=rows)
 
-        wa_t, wb_raw, pos_t = {}, {}, []
+        wa_t, wb_raw, w_t, pos_t = {}, {}, {}, []
 
         def load_wa(e):
-            wa_t[e] = at(LATE, [P, PASSES, H], I32, "wa4") if e == 4 else own([P, PASSES, H], I32, f"wa{e}")
+            wa_t[e] = at(LAST_WA, [P, PASSES, H], I32, "wa5") if e == E - 1 else own([P, PASSES, H], I32, f"wa{e}")
             nc.sync.dma_start(out=wa_t[e][:], in_=wa_src[e])
 
         def load_wb(pair):
-            wb_raw[pair] = own([P, 2, 4 * N], F32, f"wb_raw{pair}")
+            if pair == 2:
+                wb_raw[pair] = at(LAST_WB, [P, 2, 4 * N], F32, "wb_raw2")
+            else:
+                wb_raw[pair] = own([P, 2, 4 * N], F32, f"wb_raw{pair}")
             nc.sync.dma_start(out=wb_raw[pair][:], in_=wb_src[pair])
 
-        dense = [own([P, H], U8, f"dense{g}") for g in range(2)]
-        load_planes(dense[0], slice(0, 8), range(4), nc.scalar)
+        def load_w(part):
+            first, last = W_PARTS[part]
+            tile = own([P, (last - first) * PASSES, 2 * N], U8, f"w{part}")
+            nc.sync.dma_start(out=tile[:].bitcast(I32), in_=w_src[:, first * PASSES : last * PASSES, :])
+            for e in range(first, last):
+                w_t[e] = tile[:, (e - first) * PASSES : (e - first + 1) * PASSES, :]
+
+        dense = [own([P, H], U8, "dense0"), at(DENSE_SECOND, [P, H], U8, "dense1")]
+        load_planes(dense[0], slice(0, 8), nc.scalar)
         load_xs(nc.sync, 1, 0, 2)
         load_xs(nc.sync, 2, 0, 2)
         x_t = own([P, PASSES, T], I32, "x_t")
@@ -94,14 +113,25 @@ def tile_moe_elr_silu_kernel(
         nc.sync.dma_start(out=wa_first[:], in_=wa_src[0, :, 0, :])
         wa_t[0] = own([P, PASSES - 1, H], I32, "wa0")
         nc.sync.dma_start(out=wa_t[0][:], in_=wa_src[0, :, 1:, :])
-        raised = [zeroed([P, H], f"raised{g}") for g in range(2)]
+        raised = [zeroed([P, H], "raised0", RAISED_FIRST), zeroed([P, H], "raised1", RAISED_SECOND)]
         odd = zeroed([P, H], "odd")
         ws = zeroed([P, E * PASSES, N], "ws")
         shifted = zeroed([P, PASSES - 1, SLOTS], "shifted")
         warm = own([P, 1], F32, "warm")
-        nc.scalar.activation(out=warm[:], in_=raised[1][:, 0:4].bitcast(F32), func=SILU)
+        nc.scalar.activation(out=warm[:], in_=odd[:, 0:4].bitcast(F32), func=SILU)
         ident = own([P, P], F32, "ident")
         make_identity(nc, ident[:])
+        warm_sum = psum.tile([P, C], F32, name="warm_sum", tag="bank7")
+        for step in range(8):
+            nc.tensor.matmul_mx(
+                out=warm_sum[:],
+                lhsT=dense[0][:].bitcast(FP8X4),
+                lhsT_scale=dense[0][:, 0:P],
+                rhs=dense[0][:].bitcast(FP4X4),
+                rhs_scale=dense[0][:, 0:C],
+                start=True,
+                stop=True,
+            )
 
         def raise_planes(g):
             nc.sync.dma_start(out=raised[g][0 : P - 16, :].bitcast(I32), in_=dense[g][16:P, :].bitcast(I32))
@@ -113,12 +143,10 @@ def tile_moe_elr_silu_kernel(
         load_wa(3)
         load_planes(dense[1], slice(9, 17))
         load_wa(4)
-        load_wa(5)
         raise_planes(1)
-        load_wb(0)
-        load_wb(1)
-        load_wb(2)
-        w_t = own([P, E * PASSES, 2 * N], U8, "w_t")
+        for r in range(4):
+            nc.sync.dma_start(out=ws[r:P:32, :, :].bitcast(I32), in_=ws_src[r])
+        load_w(0)
 
         def wa_plane(e, s):
             group, place = divmod(e * PASSES + s, 9)
@@ -129,7 +157,7 @@ def tile_moe_elr_silu_kernel(
         y_all = own([P, SLOTS], F32, "y_all")
         groups = [(e, e + 1) for e in range(E)]
         planes_t = own([P, SLOTS], U8, "planes")
-        xs_later = own([P, BYTE_WINDOW], U8, "xs_later")
+        xs_later = own([P, T], U8, "xs_later")
         words_first = own([P, C], U32, "words_first")
         words_later = at(0, [P, E * PASSES - 1, C], U32, "words_later")
         planes, words, moved = {}, {}, {}
@@ -163,14 +191,23 @@ def tile_moe_elr_silu_kernel(
                 return wa_t[e][:, s, :]
             return wa_first[:] if s == 0 else wa_t[0][:, s - 1, :]
 
+        h_sums = {}
+
+        def silu(e, block):
+            if (e, block) in HELD_ROWS:
+                h_rows[e, block] = at(HELD_ROWS[e, block], [P, H], BF16, f"h_rows{e}_{block}")
+            else:
+                h_rows[e, block] = own([P, H], BF16, f"h_rows{e}_{block}")
+            nc.scalar.activation(
+                out=h_rows[e, block][:].rearrange("p (v m d) -> p v m d", v=2, d=2),
+                in_=h_sums[e][block][:].rearrange("p (m v d) -> p v m d", v=2, d=2),
+                func=SILU,
+            )
+
         def hidden(e):
-            sums = [psum.tile([P, H], F32, name=f"h{e}_{b}", tag=f"bank{(2 * e + b) % 8}") for b in range(2)]
-            order = [(b, s) for b in range(2) for s in range(PASSES)]
-            if e == 0:
-                order = sorted(order, key=lambda step: step[1])
-            for block, s in order:
-                if e >= 2 and (block, s) == (1, 0):
-                    turn(e - 2)
+            sums = [psum.tile([P, H], F32, name=f"h{e}_{b}", tag=f"bank{2 * (e % 3) + b}") for b in range(2)]
+            h_sums[e] = sums
+            for s, block in [(s, b) for s in range(PASSES) for b in range(2)]:
                 nc.tensor.matmul_mx(
                     out=sums[block][:],
                     lhsT=words[e, s][:, block * P : (block + 1) * P].bitcast(FP8X4),
@@ -180,17 +217,14 @@ def tile_moe_elr_silu_kernel(
                     start=(s == 0),
                     stop=(s == PASSES - 1),
                 )
-                if s == PASSES - 1:
-                    h_rows[e, block] = own([P, H], BF16, f"h_rows{e}_{block}")
-                    nc.scalar.activation(
-                        out=h_rows[e, block][:].rearrange("p (v m d) -> p v m d", v=2, d=2),
-                        in_=sums[block][:].rearrange("p (m v d) -> p v m d", v=2, d=2),
-                        func=SILU,
-                    )
+                if (e, s, block) in ((2, 1, 1), (4, 0, 1)):
+                    silu(e - 1, 1)
+                if s == PASSES - 1 and (e, block) not in DEFERRED:
+                    silu(e, block)
 
         def turn(e):
-            turned = psum.tile([P, 2, 2, P], F32, name=f"t{e}", tag=f"bank{(2 * e + 2) % 8}")
-            for block in range(2):
+            turned = psum.tile([P, 2, 2, P], F32, name=f"t{e}", tag=f"bank{TURN_BANKS[e]}")
+            for block in (1, 0):
                 for v in range(2):
                     half_row = h_rows[e, block][:].bitcast(F32)[:, v * P : (v + 1) * P]
                     nc.tensor.transpose(turned[:, block, v, :], half_row, ident[:])
@@ -200,85 +234,113 @@ def tile_moe_elr_silu_kernel(
                 in_=turned[:].rearrange("p g v j -> p g j v"),
             )
 
-        def cast_wb(e):
-            wb_grouped[e] = own([P, 2 * N * 4], BF16, f"wb_bf{e}")
+        def cast_wb(pair):
+            wb_grouped[pair] = own([P, 2 * N * 4], BF16, f"wb_bf{pair}")
             nc.vector.tensor_copy(
-                out=wb_grouped[e][:].rearrange("p (e c m j) -> p e c j m", e=2, m=4, j=4),
-                in_=wb_raw[e // 2][:].rearrange("p e (j c m) -> p e c j m", m=4, j=4),
+                out=wb_grouped[pair][:].rearrange("p (e c m j) -> p e c j m", e=2, m=4, j=4),
+                in_=wb_raw[pair][:].rearrange("p e (j c m) -> p e c j m", m=4, j=4),
             )
 
-        def quantise(values, width, name, offset=None):
-            codes = at(offset, [P, width], U32, f"{name}_codes") if offset else own([P, width], U32, f"{name}_codes")
-            plane = own([P, width], U8, f"{name}_plane")
-            nc.vector.quantize_mx(out=codes[:].bitcast(FP8X4), scales=plane[:], in_=values[:])
+        def quantise(values, codes, name):
+            plane = own([P, C], U8, f"{name}_plane")
+            nc.vector.quantize_mx(out=codes.bitcast(FP8X4), scales=plane[:], in_=values[:])
             return codes, plane
 
-        def results(e):
-            if e in wb_grouped:
-                width = 2 * N
-                codes, plane = quantise(wb_grouped[e], width, f"wb{e}")
-                for n0 in range(0, width, N):
-                    wb_quantised[e + n0 // N] = (codes[:, n0 : n0 + N], plane[:, n0 : n0 + N])
-            wb_codes, wb_plane = wb_quantised[e]
-            h_codes, h_plane = quantise(h_grouped[e], C, f"h{e}")
-            y_sum = psum.tile([P, C], F32, name=f"y{e}", tag=f"bank{(5, 6, 7, 0, 1, 3)[e]}")
+        y_sums, y_cols, h_quantised = {}, {}, {}
+        y_group = {e: group for group in Y_GROUPS for e in group}
+
+        def frozen(e):
+            group = y_group[e]
+            if e == group[0]:
+                bank = Y_BANKS[Y_GROUPS.index(group)]
+                y_sums[group] = psum.tile([P, len(group) * C], F32, name=f"y{e}", tag=f"bank{bank}")
+            y_cols[e] = y_sums[group][:, (e - group[0]) * C : (e - group[0] + 1) * C]
             for s in range(PASSES):
                 nc.tensor.matmul_mx(
-                    out=y_sum[:],
-                    lhsT=w_t[:, e * PASSES + s, :].bitcast(FP4X4),
+                    out=y_cols[e],
+                    lhsT=w_t[e][:, s, :].bitcast(FP4X4),
                     lhsT_scale=ws[:, e * PASSES + s, :],
                     rhs=words[e, s].bitcast(FP8X4),
                     rhs_scale=planes[e] if s == 0 else moved[e][:, s - 1, :],
-                    start=(s == 0),
+                    start=(s == 0 and e == group[0]),
                     stop=False,
                 )
+
+        def adapter(e):
+            wb_codes, wb_plane = wb_quantised[e // 2]
+            h_codes, h_plane = h_quantised[e]
+            cols = slice((e % 2) * N, (e % 2 + 1) * N)
+            group = y_group[e]
             nc.tensor.matmul_mx(
-                out=y_sum[:],
-                lhsT=wb_codes.bitcast(FP8X4),
-                lhsT_scale=wb_plane,
-                rhs=h_codes[:].bitcast(FP8X4),
+                out=y_cols[e],
+                lhsT=wb_codes[:, cols].bitcast(FP8X4),
+                lhsT_scale=wb_plane[:, cols],
+                rhs=h_codes.bitcast(FP8X4),
                 rhs_scale=h_plane[:],
                 start=False,
-                stop=True,
+                stop=(e == group[-1]),
             )
-            nc.scalar.copy(out=y_all[:, e * C : (e + 1) * C], in_=y_sum[:])
+            if e == E - 2:
+                nc.vector.tensor_copy(out=y_all[:, e * C : (e + 1) * C], in_=y_sums[group][:])
+            elif e == group[-1]:
+                nc.scalar.copy(out=y_all[:, group[0] * C : (e + 1) * C], in_=y_sums[group][:])
 
-        gates = own([P, TOP, T], F32, "gates")
+        gate_t = own([P, TOP, T], F32, "gate_t")
+        gates = [gate_t[:, choice, :] for choice in range(TOP)]
         for e in range(E):
             if e == 0:
                 gather_words(0, 0)
                 gather_bytes(0)
                 nc.vector.tensor_copy(xs_later[:].bitcast(I32), xs[:].bitcast(I32))
-            else:
+            elif e < E - 1:
                 gather_bytes(e)
             if e == 2:
+                load_wa(5)
                 shift(slice(0, HALF))
-                for r in range(4):
-                    nc.sync.dma_start(out=ws[r:P:32, :, :].bitcast(I32), in_=ws_src[r])
-                nc.sync.dma_start(out=w_t[:].bitcast(I32), in_=w_src)
-            if e == 5:
+                load_wb(0)
+                load_wb(1)
+            if e == E - 2:
+                gather_bytes(E - 1)
                 shift(slice(HALF, SLOTS))
+                load_wb(2)
+                load_w(1)
                 for choice, pos in enumerate((pos1, pos2, pos3)):
                     pos_t.append(held.tile([P, T // 16], U16, name=f"pos_t{choice}"))
                     nc.sync.dma_start(pos_t[choice][:], pos)
-                nc.sync.dma_start(out=gates[:], in_=gate.rearrange("r p t -> p r t"))
+                nc.sync.dma_start(out=gate_t[:], in_=gate.rearrange("r p t -> p r t"))
             for s in range(1 if e == 0 else 0, PASSES):
                 gather_words(e, s)
             hidden(e)
-        turn(E - 2)
-        cast_wb(0)
-        cast_wb(2)
-        cast_wb(4)
-        results(0)
-        results(1)
-        turn(E - 1)
-        for e in range(2, E):
-            results(e)
+            if e in (2, 4):
+                turn(e - 2)
+                turn(e - 1)
+        late_codes = own([P, 4, C], U32, "late_codes")
+        for pair, experts in enumerate(((0, 1), (2, 3), ())):
+            cast_wb(pair)
+            for e in experts:
+                h_quantised[e] = quantise(h_grouped[e], late_codes[:, e, :], f"h{e}")
+            wb_quantised[pair] = quantise(wb_grouped[pair], own([P, C], U32, f"wb{pair}_codes")[:], f"wb{pair}")
+        for e in (2, 0, 1):
+            frozen(e)
+        turn(4)
+        turn(5)
+        for e in (4, 5):
+            codes = at(LAST_WB + (e - 4) * C * 4, [P, C], U32, f"h{e}_codes")
+            h_quantised[e] = quantise(h_grouped[e], codes[:], f"h{e}")
+        adapter(0)
+        adapter(1)
+        frozen(3)
+        adapter(2)
+        adapter(3)
+        frozen(4)
+        frozen(5)
+        adapter(4)
+        adapter(5)
 
         halves = [slice(0, T // 2), slice(T // 2, T)]
         picked = [own([P, T], F32, f"picked{choice}") for choice in range(1, TOP)]
         weighted = [own([P, T], F32, f"weighted{choice}") for choice in range(TOP)]
-        nc.vector.tensor_tensor(weighted[0][:], y_all[:].indirect(pos_t[0][:]), gates[:, 0, :], MULT)
+        nc.vector.tensor_tensor(weighted[0][:], y_all[:].indirect(pos_t[0][:]), gates[0], MULT)
         nc.scalar.activation(out=picked[0][:], in_=y_all[:].indirect(pos_t[1][:]), func=COPY)
         for tokens in halves:
             nc.scalar.activation(
@@ -287,10 +349,10 @@ def tile_moe_elr_silu_kernel(
                 func=COPY,
             )
         two = own([P, T], F32, "two")
-        nc.vector.tensor_tensor(weighted[1][:], picked[0][:], gates[:, 1, :], MULT)
-        nc.vector.tensor_tensor(weighted[2][:, halves[0]], picked[1][:, halves[0]], gates[:, 2, halves[0]], MULT)
+        nc.vector.tensor_tensor(weighted[1][:], picked[0][:], gates[1], MULT)
+        nc.vector.tensor_tensor(weighted[2][:, halves[0]], picked[1][:, halves[0]], gates[2][:, halves[0]], MULT)
         nc.vector.tensor_tensor(two[:], weighted[0][:], weighted[1][:], ADD)
-        nc.vector.tensor_tensor(weighted[2][:, halves[1]], picked[1][:, halves[1]], gates[:, 2, halves[1]], MULT)
+        nc.vector.tensor_tensor(weighted[2][:, halves[1]], picked[1][:, halves[1]], gates[2][:, halves[1]], MULT)
         for part, tokens in enumerate(halves):
             total = own([P, T // 2], F32, f"total{part}")
             nc.vector.tensor_tensor(total[:], two[:, tokens], weighted[2][:, tokens], ADD)

@@ -28,11 +28,12 @@ RAISED_FIRST = LAST_WA + (E + 1) * C * 4 + 768
 DENSE_SECOND = RAISED_FIRST + 256 + 2 * H
 RAISED_SECOND = DENSE_SECOND + 2 * H + 768
 LAST_WB = RAISED_SECOND + 256 + 2 * H
-TURN_BANKS = (3, 6, 1, 7, 5, 6)
-HELD_ROWS = {(1, 1): RAISED_FIRST - 768, (2, 0): RAISED_FIRST + 256, (3, 1): DENSE_SECOND}
-DEFERRED = ((1, 1), (3, 1))
-W_PARTS = ((0, 3), (3, 6))
-HALF = SLOTS // 2
+DENSE_FIRST = LAST_WB + 4096
+TURN_BANKS = (6, 3, 1, 7, 5, 6)
+HELD_ROWS = {(1, 1): RAISED_FIRST - 768, (2, 0): RAISED_FIRST + 256, (3, 1): DENSE_SECOND, (0, 1): DENSE_FIRST}
+DEFERRED = ((0, 1), (1, 1), (3, 1))
+W_PARTS = ((0, 4), (4, 6))
+EARLY_SLOTS = 4 * C
 Y_GROUPS = ((0, 1), (2, 3), (4,), (5,))
 Y_BANKS = (3, 2, 0, 1)
 
@@ -100,7 +101,7 @@ def tile_moe_elr_silu_kernel(
             for e in range(first, last):
                 w_t[e] = tile[:, (e - first) * PASSES : (e - first + 1) * PASSES, :]
 
-        dense = [own([P, H], U8, "dense0"), at(DENSE_SECOND, [P, H], U8, "dense1")]
+        dense = [at(DENSE_FIRST, [P, H], U8, "dense0"), at(DENSE_SECOND, [P, H], U8, "dense1")]
         load_planes(dense[0], slice(0, 8), nc.scalar)
         load_xs(nc.sync, 1, 0, 2)
         load_xs(nc.sync, 2, 0, 2)
@@ -121,17 +122,6 @@ def tile_moe_elr_silu_kernel(
         nc.scalar.activation(out=warm[:], in_=odd[:, 0:4].bitcast(F32), func=SILU)
         ident = own([P, P], F32, "ident")
         make_identity(nc, ident[:])
-        warm_sum = psum.tile([P, C], F32, name="warm_sum", tag="bank7")
-        for step in range(8):
-            nc.tensor.matmul_mx(
-                out=warm_sum[:],
-                lhsT=dense[0][:].bitcast(FP8X4),
-                lhsT_scale=dense[0][:, 0:P],
-                rhs=dense[0][:].bitcast(FP4X4),
-                rhs_scale=dense[0][:, 0:C],
-                start=True,
-                stop=True,
-            )
 
         def raise_planes(g):
             nc.sync.dma_start(out=raised[g][0 : P - 16, :].bitcast(I32), in_=dense[g][16:P, :].bitcast(I32))
@@ -217,7 +207,7 @@ def tile_moe_elr_silu_kernel(
                     start=(s == 0),
                     stop=(s == PASSES - 1),
                 )
-                if (e, s, block) in ((2, 1, 1), (4, 0, 1)):
+                if (e, s, block) in ((1, 0, 1), (2, 1, 1), (4, 0, 1)):
                     silu(e - 1, 1)
                 if s == PASSES - 1 and (e, block) not in DEFERRED:
                     silu(e, block)
@@ -292,17 +282,16 @@ def tile_moe_elr_silu_kernel(
                 gather_words(0, 0)
                 gather_bytes(0)
                 nc.vector.tensor_copy(xs_later[:].bitcast(I32), xs[:].bitcast(I32))
-            elif e < E - 1:
+            else:
                 gather_bytes(e)
-            if e == 2:
+            if e == 3:
                 load_wa(5)
-                shift(slice(0, HALF))
+                shift(slice(0, EARLY_SLOTS))
                 load_wb(0)
                 load_wb(1)
-            if e == E - 2:
-                gather_bytes(E - 1)
-                shift(slice(HALF, SLOTS))
+            if e == E - 1:
                 load_wb(2)
+                shift(slice(EARLY_SLOTS, SLOTS))
                 load_w(1)
                 for choice, pos in enumerate((pos1, pos2, pos3)):
                     pos_t.append(held.tile([P, T // 16], U16, name=f"pos_t{choice}"))
@@ -311,8 +300,9 @@ def tile_moe_elr_silu_kernel(
             for s in range(1 if e == 0 else 0, PASSES):
                 gather_words(e, s)
             hidden(e)
-            if e in (2, 4):
-                turn(e - 2)
+            if e == 4:
+                turn(2)
+            if e in (1, 2, 4):
                 turn(e - 1)
         late_codes = own([P, 4, C], U32, "late_codes")
         for pair, experts in enumerate(((0, 1), (2, 3), ())):

@@ -48,10 +48,10 @@ def tile_moe_elr_silu_kernel(
         psum = ctx.enter_context(tc.psum_pool(name="psum", bufs=1))
 
         def own(shape, dtype, name, tag=None):
-            return held.tile(shape, dtype, name=name, tag=tag or name, align_bytes=64)
+            return held.tile(shape, dtype, name=name, tag=tag or name, align_bytes=256)
 
         def at(offset, shape, dtype, name):
-            return placed.tile(shape, dtype, name=name, tag=name, align_bytes=64, offset=offset)
+            return placed.tile(shape, dtype, name=name, tag=name, align_bytes=256, offset=offset)
 
         def zeroed(shape, name, offset=None):
             plane = at(offset, shape, U8, name) if offset else own(shape, U8, name)

from contextlib import ExitStack

import concourse.mybir as mybir
from concourse.masks import make_identity

K, T, E, C, H, N, TOP = 1536, 512, 6, 256, 512, 128, 3
P = 128
PASSES = K // 512
SLOTS = E * C
FLOPS = 2 * SLOTS * (K * (H + N) + H * N)

F32 = mybir.dt.float32
BF16 = mybir.dt.bfloat16
I32 = mybir.dt.int32
U32 = mybir.dt.uint32
U16 = mybir.dt.uint16
U8 = mybir.dt.uint8
FP8X4 = mybir.dt.float8_e4m3fn_x4
FP4X4 = mybir.dt.float4_e2m1fn_x4
SILU = mybir.ActivationFunctionType.Silu
COPY = mybir.ActivationFunctionType.Copy
MULT = mybir.AluOpType.mult
ADD = mybir.AluOpType.add

PLANE_ROWS = 100
LAST_WA = (E * PASSES - 1) * C * 4
RAISED_FIRST = LAST_WA + (E + 1) * C * 4 + 768
DENSE_SECOND = RAISED_FIRST + 256 + 2 * H
RAISED_SECOND = DENSE_SECOND + 2 * H + 768
LAST_WB = RAISED_SECOND + 256 + 2 * H
DENSE_FIRST = LAST_WB + 4096
TURN_BANKS = (6, 3, 1, 7, 5, 6)
HELD_ROWS = {(1, 1): RAISED_FIRST - 768, (2, 0): RAISED_FIRST + 256, (3, 1): DENSE_SECOND, (0, 1): DENSE_FIRST}
DEFERRED = ((0, 1), (1, 1), (3, 1))
W_PARTS = ((0, 4), (4, 6))
EARLY_SLOTS = 4 * C
Y_GROUPS = ((0, 1), (2, 3), (4,), (5,))
Y_BANKS = (3, 2, 0, 1)


def tile_moe_elr_silu_kernel(
    tc, x_words, x_scales, w_words, w_scales, wa_words, wa_scales, wb, gate, offs, pos1, pos2, pos3, out
):
    nc = tc.nc
    with ExitStack() as ctx:
        held = ctx.enter_context(tc.tile_pool(name="held", bufs=1))
        placed = ctx.enter_context(tc.tile_pool(name="placed", bufs=1))
        psum = ctx.enter_context(tc.psum_pool(name="psum", bufs=1))

        def own(shape, dtype, name, tag=None):
            return held.tile(shape, dtype, name=name, tag=tag or name, align_bytes=256)

        def at(offset, shape, dtype, name):
            return placed.tile(shape, dtype, name=name, tag=name, align_bytes=256, offset=offset)

        def zeroed(shape, name, offset=None):
            plane = at(offset, shape, U8, name) if offset else own(shape, U8, name)
            nc.vector.memset(plane[:].bitcast(I32), 0)
            return plane

        was_src = wa_scales.bitcast(I32).rearrange("e s (q r) c -> q (e s) r c", r=4)
        wa_src = wa_words.rearrange("e s p i d -> e p s (i d)").bitcast(I32)
        xw_src = x_words.rearrange("s p t d -> p s (t d)").bitcast(I32)
        xs_src = x_scales.bitcast(I32).rearrange("s (q r) c -> q s r c", r=4)
        w_src = w_words.bitcast(I32).rearrange("e s p c -> p (e s) c")
        wb_src = wb.rearrange("(g e) (p j) n -> g p e (j n)", e=2, j=4)
        ws_src = w_scales.bitcast(I32).rearrange("e s (q r) c -> r q (e s) c", r=4)

        xs = at(0, [P, T], U8, "xs")
        nc.gpsimd.memset(xs[:].bitcast(I32), 0)
        offs_t = held.tile([P, SLOTS // 16], U16, name="offs_t")
        nc.sync.dma_start(offs_t[:], offs)

        def load_xs(queue, q, s0, s1):
            queue.dma_start(out=xs[32 * q + 4 * s0 : 32 * q + 4 * s1, :].bitcast(I32), in_=xs_src[q, s0:s1])

        load_xs(nc.gpsimd, 0, 0, 3)

        def load_planes(plane, numbers, queue=nc.sync):
            for q in range(4):
                rows = was_src[q, numbers]
                queue.dma_start(out=plane[32 * q : 32 * q + 4 * rows.shape[0], :].bitcast(I32), in_=rows)

        wa_t, wb_raw, w_t, pos_t = {}, {}, {}, []

        def load_wa(e):
            wa_t[e] = at(LAST_WA, [P, PASSES, H], I32, "wa5") if e == E - 1 else own([P, PASSES, H], I32, f"wa{e}")
            nc.sync.dma_start(out=wa_t[e][:], in_=wa_src[e])

        def load_wb(pair):
            if pair == 2:
                wb_raw[pair] = at(LAST_WB, [P, 2, 4 * N], F32, "wb_raw2")
            else:
                wb_raw[pair] = own([P, 2, 4 * N], F32, f"wb_raw{pair}")
            nc.sync.dma_start(out=wb_raw[pair][:], in_=wb_src[pair])

        def load_w(part):
            first, last = W_PARTS[part]
            tile = own([P, (last - first) * PASSES, 2 * N], U8, f"w{part}")
            nc.sync.dma_start(out=tile[:].bitcast(I32), in_=w_src[:, first * PASSES : last * PASSES, :])
            for e in range(first, last):
                w_t[e] = tile[:, (e - first) * PASSES : (e - first + 1) * PASSES, :]

        dense = [at(DENSE_FIRST, [P, H], U8, "dense0"), at(DENSE_SECOND, [P, H], U8, "dense1")]
        load_planes(dense[0], slice(0, 8), nc.scalar)
        load_xs(nc.sync, 1, 0, 2)
        load_xs(nc.sync, 2, 0, 2)
        x_t = own([P, PASSES, T], I32, "x_t")
        nc.sync.dma_start(out=x_t[:], in_=xw_src)
        load_xs(nc.sync, 3, 0, 2)
        for q in range(1, 4):
            load_xs(nc.sync, q, 2, 3)
        wa_first = own([P, H], I32, "wa_first")
        nc.sync.dma_start(out=wa_first[:], in_=wa_src[0, :, 0, :])
        wa_t[0] = own([P, PASSES - 1, H], I32, "wa0")
        nc.sync.dma_start(out=wa_t[0][:], in_=wa_src[0, :, 1:, :])
        raised = [zeroed([P, H], "raised0", RAISED_FIRST), zeroed([P, H], "raised1", RAISED_SECOND)]
        odd = zeroed([P, H], "odd")
        ws = zeroed([P, E * PASSES, N], "ws")
        shifted = zeroed([P, PASSES - 1, SLOTS], "shifted")
        warm = own([P, 1], F32, "warm")
        nc.scalar.activation(out=warm[:], in_=odd[:, 0:4].bitcast(F32), func=SILU)
        ident = own([P, P], F32, "ident")
        make_identity(nc, ident[:])

        def raise_planes(g):
            nc.sync.dma_start(out=raised[g][0 : P - 16, :].bitcast(I32), in_=dense[g][16:P, :].bitcast(I32))

        load_wa(1)
        raise_planes(0)
        load_wa(2)
        load_planes(odd, slice(8, 18, 9))
        load_wa(3)
        load_planes(dense[1], slice(9, 17))
        load_wa(4)
        raise_planes(1)
        for r in range(4):
            nc.sync.dma_start(out=ws[r:P:32, :, :].bitcast(I32), in_=ws_src[r])
        load_w(0)

        def wa_plane(e, s):
            group, place = divmod(e * PASSES + s, 9)
            if place == 8:
                return odd[4 * group :, :]
            return (dense if place < 4 else raised)[group][4 * (place % 4) :, :]

        y_all = own([P, SLOTS], F32, "y_all")
        groups = [(e, e + 1) for e in range(E)]
        planes_t = own([P, SLOTS], U8, "planes")
        xs_later = own([P, T], U8, "xs_later")
        words_first = own([P, C], U32, "words_first")
        words_later = at(0, [P, E * PASSES - 1, C], U32, "words_later")
        planes, words, moved = {}, {}, {}
        for e in range(E):
            planes[e] = planes_t[:, e * C : (e + 1) * C]
            moved[e] = shifted[:, :, e * C : (e + 1) * C]
            for s in range(PASSES):
                words[e, s] = words_later[:, e * PASSES + s - 1, :] if e + s else words_first[:]
        h_rows, h_grouped, wb_grouped, wb_quantised = {}, {}, {}, {}

        def offsets(first, last):
            return offs_t[:, first // 16 : last // 16]

        def gather_bytes(g):
            e0, e1 = groups[g]
            window = xs_later if g else xs
            nc.vector.tensor_copy(planes_t[:, e0 * C : e1 * C], window[:].indirect(offsets(e0 * C, e1 * C)))

        def shift(cols):
            for s in range(1, PASSES):
                nc.sync.dma_start(
                    out=shifted[0:PLANE_ROWS, s - 1, cols].bitcast(I32),
                    in_=planes_t[4 * s : 4 * s + PLANE_ROWS, cols].bitcast(I32),
                )

        def gather_words(e, s):
            nc.vector.tensor_copy(words[e, s], x_t[:, s, :].bitcast(U32).indirect(offsets(e * C, (e + 1) * C)))

        def wa_pass(e, s):
            if e > 0:
                return wa_t[e][:, s, :]
            return wa_first[:] if s == 0 else wa_t[0][:, s - 1, :]

        h_sums = {}

        def silu(e, block):
            if (e, block) in HELD_ROWS:
                h_rows[e, block] = at(HELD_ROWS[e, block], [P, H], BF16, f"h_rows{e}_{block}")
            else:
                h_rows[e, block] = own([P, H], BF16, f"h_rows{e}_{block}")
            nc.scalar.activation(
                out=h_rows[e, block][:].rearrange("p (v m d) -> p v m d", v=2, d=2),
                in_=h_sums[e][block][:].rearrange("p (m v d) -> p v m d", v=2, d=2),
                func=SILU,
            )

        def hidden(e):
            sums = [psum.tile([P, H], F32, name=f"h{e}_{b}", tag=f"bank{2 * (e % 3) + b}") for b in range(2)]
            h_sums[e] = sums
            for s, block in [(s, b) for s in range(PASSES) for b in range(2)]:
                nc.tensor.matmul_mx(
                    out=sums[block][:],
                    lhsT=words[e, s][:, block * P : (block + 1) * P].bitcast(FP8X4),
                    lhsT_scale=planes[e][4 * s :, block * P : (block + 1) * P],
                    rhs=wa_pass(e, s).bitcast(FP8X4),
                    rhs_scale=wa_plane(e, s),
                    start=(s == 0),
                    stop=(s == PASSES - 1),
                )
                if (e, s, block) in ((1, 0, 1), (2, 1, 1), (4, 0, 1)):
                    silu(e - 1, 1)
                if s == PASSES - 1 and (e, block) not in DEFERRED:
                    silu(e, block)

        def turn(e):
            turned = psum.tile([P, 2, 2, P], F32, name=f"t{e}", tag=f"bank{TURN_BANKS[e]}")
            for block in (1, 0):
                for v in range(2):
                    half_row = h_rows[e, block][:].bitcast(F32)[:, v * P : (v + 1) * P]
                    nc.tensor.transpose(turned[:, block, v, :], half_row, ident[:])
            h_grouped[e] = own([P, 4 * C], BF16, f"hb{e}")
            nc.scalar.copy(
                out=h_grouped[e][:].bitcast(F32).rearrange("p (g j v) -> p g j v", v=2, j=P),
                in_=turned[:].rearrange("p g v j -> p g j v"),
            )

        def cast_wb(pair):
            wb_grouped[pair] = own([P, 2 * N * 4], BF16, f"wb_bf{pair}")
            nc.vector.tensor_copy(
                out=wb_grouped[pair][:].rearrange("p (e c m j) -> p e c j m", e=2, m=4, j=4),
                in_=wb_raw[pair][:].rearrange("p e (j c m) -> p e c j m", m=4, j=4),
            )

        def quantise(values, codes, name):
            plane = own([P, C], U8, f"{name}_plane")
            nc.vector.quantize_mx(out=codes.bitcast(FP8X4), scales=plane[:], in_=values[:])
            return codes, plane

        y_sums, y_cols, h_quantised = {}, {}, {}
        y_group = {e: group for group in Y_GROUPS for e in group}

        def frozen(e):
            group = y_group[e]
            if e == group[0]:
                bank = Y_BANKS[Y_GROUPS.index(group)]
                y_sums[group] = psum.tile([P, len(group) * C], F32, name=f"y{e}", tag=f"bank{bank}")
            y_cols[e] = y_sums[group][:, (e - group[0]) * C : (e - group[0] + 1) * C]
            for s in range(PASSES):
                nc.tensor.matmul_mx(
                    out=y_cols[e],
                    lhsT=w_t[e][:, s, :].bitcast(FP4X4),
                    lhsT_scale=ws[:, e * PASSES + s, :],
                    rhs=words[e, s].bitcast(FP8X4),
                    rhs_scale=planes[e] if s == 0 else moved[e][:, s - 1, :],
                    start=(s == 0 and e == group[0]),
                    stop=False,
                )

        def adapter(e):
            wb_codes, wb_plane = wb_quantised[e // 2]
            h_codes, h_plane = h_quantised[e]
            cols = slice((e % 2) * N, (e % 2 + 1) * N)
            group = y_group[e]
            nc.tensor.matmul_mx(
                out=y_cols[e],
                lhsT=wb_codes[:, cols].bitcast(FP8X4),
                lhsT_scale=wb_plane[:, cols],
                rhs=h_codes.bitcast(FP8X4),
                rhs_scale=h_plane[:],
                start=False,
                stop=(e == group[-1]),
            )
            if e == E - 2:
                nc.vector.tensor_copy(out=y_all[:, e * C : (e + 1) * C], in_=y_sums[group][:])
            elif e == group[-1]:
                nc.scalar.copy(out=y_all[:, group[0] * C : (e + 1) * C], in_=y_sums[group][:])

        gate_t = own([P, TOP, T], F32, "gate_t")
        gates = [gate_t[:, choice, :] for choice in range(TOP)]
        for e in range(E):
            if e == 0:
                gather_words(0, 0)
                gather_bytes(0)
                nc.vector.tensor_copy(xs_later[:].bitcast(I32), xs[:].bitcast(I32))
            else:
                gather_bytes(e)
            if e == 3:
                load_wa(5)
                shift(slice(0, EARLY_SLOTS))
                load_wb(0)
                load_wb(1)
            if e == E - 1:
                load_wb(2)
                shift(slice(EARLY_SLOTS, SLOTS))
                load_w(1)
                for choice, pos in enumerate((pos1, pos2, pos3)):
                    pos_t.append(held.tile([P, T // 16], U16, name=f"pos_t{choice}"))
                    nc.sync.dma_start(pos_t[choice][:], pos)
                nc.sync.dma_start(out=gate_t[:], in_=gate.rearrange("r p t -> p r t"))
            for s in range(1 if e == 0 else 0, PASSES):
                gather_words(e, s)
            hidden(e)
            if e == 4:
                turn(2)
            if e in (1, 2, 4):
                turn(e - 1)
        late_codes = own([P, 4, C], U32, "late_codes")
        for pair, experts in enumerate(((0, 1), (2, 3), ())):
            cast_wb(pair)
            for e in experts:
                h_quantised[e] = quantise(h_grouped[e], late_codes[:, e, :], f"h{e}")
            wb_quantised[pair] = quantise(wb_grouped[pair], own([P, C], U32, f"wb{pair}_codes")[:], f"wb{pair}")
        for e in (2, 0, 1):
            frozen(e)
        turn(4)
        turn(5)
        for e in (4, 5):
            codes = at(LAST_WB + (e - 4) * C * 4, [P, C], U32, f"h{e}_codes")
            h_quantised[e] = quantise(h_grouped[e], codes[:], f"h{e}")
        adapter(0)
        adapter(1)
        frozen(3)
        adapter(2)
        adapter(3)
        frozen(4)
        frozen(5)
        adapter(4)
        adapter(5)

        halves = [slice(0, T // 2), slice(T // 2, T)]
        picked = [own([P, T], F32, f"picked{choice}") for choice in range(1, TOP)]
        weighted = [own([P, T], F32, f"weighted{choice}") for choice in range(TOP)]
        nc.vector.tensor_tensor(weighted[0][:], y_all[:].indirect(pos_t[0][:]), gates[0], MULT)
        nc.scalar.activation(out=picked[0][:], in_=y_all[:].indirect(pos_t[1][:]), func=COPY)
        for tokens in halves:
            nc.scalar.activation(
                out=picked[1][:, tokens],
                in_=y_all[:].indirect(pos_t[2][:, tokens.start // 16 : tokens.stop // 16]),
                func=COPY,
            )
        two = own([P, T], F32, "two")
        nc.vector.tensor_tensor(weighted[1][:], picked[0][:], gates[1], MULT)
        nc.vector.tensor_tensor(weighted[2][:, halves[0]], picked[1][:, halves[0]], gates[2][:, halves[0]], MULT)
        nc.vector.tensor_tensor(two[:], weighted[0][:], weighted[1][:], ADD)
        nc.vector.tensor_tensor(weighted[2][:, halves[1]], picked[1][:, halves[1]], gates[2][:, halves[1]], MULT)
        for part, tokens in enumerate(halves):
            total = own([P, T // 2], F32, f"total{part}")
            nc.vector.tensor_tensor(total[:], two[:, tokens], weighted[2][:, tokens], ADD)
            nc.sync.dma_start(out=out[:, tokens], in_=total[:])
